import numpy as np
import ml_dtypes


def mxq(x, axis, fmt="e4m3"):
    dtype, down = {"e4m3": (ml_dtypes.float8_e4m3fn, 7), "e5m2": (ml_dtypes.float8_e5m2, 14)}[fmt]
    v = np.moveaxis(np.asarray(x, np.float32).astype(ml_dtypes.bfloat16).astype(np.float64), axis, -1)
    blocks = v.reshape(v.shape[:-1] + (-1, 32))
    amax = np.abs(blocks).max(-1, keepdims=True)
    byte = np.maximum(np.where(amax > 0, np.frexp(amax)[1] - 1 + 127, 0) - down, 1)
    scale = np.exp2(byte - 127.0)
    codes = (blocks / scale).astype(np.float32).astype(dtype).astype(np.float64)
    return np.moveaxis((codes * scale).reshape(v.shape), -1, axis)


WIDE = False


def mx_kscale(k):
    if not WIDE:
        return np.ones(k)
    levels = np.array([10, -10, 5, -5, 0])
    if k % 512:
        return np.exp2(np.random.permutation(np.resize(levels, k // 32))).repeat(32)
    a = np.empty((k // 512, 16))
    for p in range(k // 512):
        a[p, :8] = np.random.permutation(np.resize(levels, 8))
        for g in range(8):
            far = levels[np.abs(levels - a[p, g]) >= 10]
            a[p, g + 8] = far[np.random.randint(len(far))]
    return np.exp2(a.ravel()).repeat(32)


def f64(x):
    return np.asarray(x).astype(np.float64)


def striped(idx):
    return np.tile(idx.reshape(-1, 16).T, (8, 1)).astype(np.uint16)


def unstriped(offs):
    return offs[:16].T.reshape(-1).astype(np.int64)


E2M1 = np.array([0.0, 0.5, 1.0, 1.5, 2.0, 3.0, 4.0, 6.0, -0.0, -0.5, -1.0, -1.5, -2.0, -3.0, -4.0, -6.0])


def pack_weight(w, fmt):
    k, n = w.shape
    w = f64(np.asarray(w, np.float32).astype(ml_dtypes.bfloat16)).reshape(k // 32, 32, n)
    amax = np.abs(w).max(1)
    if fmt == "e4m3":
        byte = np.frexp(amax)[1] - 1 + 127 - 7
    else:
        mant, ex = np.frexp(amax / 6.0)
        byte = np.where(mant > 0.5, ex, ex - 1) + 127
    byte = np.clip(np.where(amax > 0, byte, 1), 1, 254)
    scaled = (w * np.exp2(127.0 - byte)[:, None, :]).reshape(k, n).astype(np.float32)
    by_word = np.ascontiguousarray(scaled.reshape(k // 512, 128, 4, n).transpose(0, 1, 3, 2))
    if fmt == "e4m3":
        words = by_word.astype(ml_dtypes.float8_e4m3fn).view(np.uint8)
    else:
        c = by_word.astype(ml_dtypes.float4_e2m1fn).view(np.uint8) & 0xF
        words = (c[..., 0::2] | (c[..., 1::2] << 4)).reshape(k // 512, 128, 2 * n)
    return np.ascontiguousarray(words), np.ascontiguousarray(byte.astype(np.uint8).reshape(k // 512, 16, n))


def unpack_weight(words, scales, fmt):
    g, _, n = scales.shape
    words = np.ascontiguousarray(words).reshape(g, 128, n, -1)
    if fmt == "e4m3":
        vals = words.view(ml_dtypes.float8_e4m3fn).astype(np.float64)
    else:
        nib = np.empty((g, 128, n, 4), np.uint8)
        nib[..., 0::2] = words & 0xF
        nib[..., 1::2] = words >> 4
        vals = E2M1[nib]
    vals = vals * np.repeat(np.exp2(scales.astype(np.float64) - 127.0), 8, axis=1)[..., None]
    return vals.transpose(0, 1, 3, 2).reshape(g * 512, n)


def gelu(v):
    return 0.5 * v * (1.0 + np.tanh(np.sqrt(2.0 / np.pi) * (v + 0.044715 * v**3)))


K, T, E, C, N = 2048, 640, 15, 128, 128
TOP = 3


def by_expert(wq, xq):
    return np.concatenate([wq[e].T @ xq[:, e * C:(e + 1) * C] for e in range(E)], axis=1)


def setup_inputs():
    n = np.random.standard_normal
    s = mx_kscale(K)[:, None]
    deal = np.repeat(np.arange(E), C).reshape(TOP, T)[:, np.random.permutation(T)]
    deal = np.take_along_axis(deal, np.argsort(np.random.rand(TOP, T), axis=0), axis=0)
    for _ in range(8):
        s_, t_ = np.random.permutation(T).reshape(2, -1); r = np.random.randint(TOP, size=T // 2); x, y = deal[r, s_].copy(), deal[r, t_].copy()
        ok = ~((deal[:, s_] == y).any(0) | (deal[:, t_] == x).any(0)); deal[r[ok], s_[ok]] = y[ok]; deal[r[ok], t_[ok]] = x[ok]
    order = np.lexsort((np.random.rand(TOP * T), deal.reshape(-1)))
    slot_token = order % T; pos = np.empty(TOP * T, np.int64); pos[order] = np.arange(TOP * T); pos = pos.reshape(TOP, T)
    g = np.random.uniform(0.5, 1.5, (TOP, T)); g = g / g.sum(0)
    x = pack_weight(n((K, T)) * s, "e4m3")
    return {
        "x_words": x[0],
        "x_scales": x[1],
        "w": (n((E, K, N)) / np.sqrt(K) / s[None]).astype(np.float32),
        "b": (0.3 * n((N, E))).astype(np.float32),
        "gate": np.stack([np.tile(r, (N, 1)) for r in g]).astype(np.float32),
        "offs": striped(slot_token),
        "pos1": striped(pos[0]),
        "pos2": striped(pos[1]),
        "pos3": striped(pos[2]),
    }


def reference(x_words, x_scales, w, b, gate, offs, pos1, pos2, pos3):
    idx = unstriped(offs)
    xq = unpack_weight(x_words, x_scales, "e4m3")[:, idx]
    y = by_expert(mxq(f64(w), 1, "e4m3"), xq)
    y = gelu(y + np.repeat(f64(b), C, axis=1))
    return sum(f64(gate[r]) * y[:, unstriped(p)] for r, p in enumerate((pos1, pos2, pos3)))

@@ -1,0 +1,187 @@
+from contextlib import ExitStack
+
+import concourse.mybir as mybir
+
+K, T, E, C, N = 2048, 640, 15, 128, 128
+TOP = 3
+FLOPS = 2 * E * C * K * N
+
+F32 = mybir.dt.float32
+BF16 = mybir.dt.bfloat16
+I32 = mybir.dt.int32
+U32 = mybir.dt.uint32
+U16 = mybir.dt.uint16
+U8 = mybir.dt.uint8
+FP8X4 = mybir.dt.float8_e4m3fn_x4
+GELU = mybir.ActivationFunctionType.Gelu_apprx_tanh
+MULT = mybir.AluOpType.mult
+ADD = mybir.AluOpType.add
+
+P = 128
+PACK = 4
+PASSES = K // (P * PACK)
+STRIPE = 16
+RUN = 4
+LEAD = 3
+GROUPS = [[0]] + [[e, e + 1] for e in range(1, E, 2)]
+VEC_PASSES = [0,0,0,0,0,0,0,0,0,0,0,0,0,1,0]
+PIECES = [2,1,1,1,1,1,1,1,1,1,1,1,1,1,4]
+
+
+def tile_moe_pkd_lin_gelu_kernel(tc, x_words, x_scales, w, b, gate, offs, pos1, pos2, pos3, out):
+    nc = tc.nc
+    with ExitStack() as ctx:
+        keep = ctx.enter_context(tc.tile_pool(name="keep", bufs=1))
+        stage = ctx.enter_context(tc.tile_pool(name="stage", bufs=1))
+        raw_pool = ctx.enter_context(tc.tile_pool(name="raw", bufs=8))
+        code_pool = ctx.enter_context(tc.tile_pool(name="codes", bufs=4))
+        sg_pool = ctx.enter_context(tc.tile_pool(name="sg", bufs=3))
+        psum = ctx.enter_context(tc.psum_pool(name="psum", bufs=4))
+
+        offs_sb = keep.tile([P, E * C // STRIPE], U16, name="offs_sb")
+        nc.sync.dma_start(offs_sb[:], offs)
+
+        x_plane = keep.tile([P, T], U8, name="x_plane", align_bytes=64)
+        nc.vector.memset(x_plane[:].bitcast(I32), 0)
+
+        warm = keep.tile([P, 1], F32, name="warm")
+        nc.vector.memset(warm[:], 0.0)
+        warm_out = keep.tile([P, 1], F32, name="warm_out")
+        nc.scalar.activation(warm_out[:], warm[:], GELU)
+
+        words_hbm = x_words.rearrange("o p t r -> p o (t r)").bitcast(I32)
+        scales_hbm = x_scales.bitcast(I32)
+        x_half = [keep.tile([P, 2, T], I32, name=f"x_half{h}", align_bytes=64) for h in range(2)]
+        raw = {}
+
+        def load_x(h):
+            nc.sync.dma_start(x_half[h][:], words_hbm[:, 2 * h : 2 * h + 2, :])
+
+        def load_w(e):
+            n_pass = PASSES // PIECES[e]
+            for piece in range(PIECES[e]):
+                t = raw_pool.tile([P, n_pass, PACK, N], F32, name=f"raw{e}_{piece}", tag="raw")
+                rows = w[e, piece * n_pass * P * PACK : (piece + 1) * n_pass * P * PACK, :]
+                nc.sync.dma_start(t[:], rows.rearrange("(o p j) n -> p o j n", p=P, j=PACK))
+                raw[e, piece] = t
+
+        def load_scales():
+            for q in range(4):
+                nc.sync.dma_start(x_plane[32 * q : 32 * q + 16, :].bitcast(I32), scales_hbm[:, 4 * q : 4 * q + 4, :])
+
+        load_x(0)
+        load_x(1)
+        load_w(0)
+        load_scales()
+        load_w(1)
+        b_sb = keep.tile([P, E], F32, name="b_sb")
+        nc.sync.dma_start(b_sb[:], b)
+        pos_sb = []
+        y = keep.tile([P, E * C], F32, name="y")
+
+        slot_words = {}
+        slot_scales = {}
+
+        def list_slice(g):
+            return offs_sb[:, GROUPS[g][0] * C // STRIPE : (GROUPS[g][-1] + 1) * C // STRIPE]
+
+        def gather_words(g, h, tag):
+            t = stage.tile([P, 2, len(GROUPS[g]) * C], U32, name=f"xg{g}_{h}", tag=tag, align_bytes=64)
+            for o in range(2):
+                nc.vector.tensor_copy(t[:, o, :], x_half[h][:, o, :].bitcast(U32).indirect(list_slice(g)))
+            slot_words[g, h] = t
+
+        def gather_scales(g):
+            t = sg_pool.tile([P, len(GROUPS[g]) * C], U8, name=f"sg{g}", tag="sg", align_bytes=64)
+            nc.vector.tensor_copy(t[:], x_plane[:].indirect(list_slice(g)))
+            slot_scales[g] = t
+
+        def cast(engine_copy, dst, src):
+            engine_copy(
+                dst.rearrange("p o (c i) j -> p o c j i", i=RUN),
+                src.rearrange("p o j (c i) -> p o c j i", i=RUN),
+            )
+
+        first = [g for g in range(len(GROUPS)) if GROUPS[g][0] < LEAD]
+        later = [(g, h) for g in range(len(first), len(GROUPS)) for h in range(2)]
+        for h in range(2):
+            for g in first:
+                gather_words(g, h, f"first{g}_{h}")
+        for g in first:
+            gather_scales(g)
+
+        for e in range(E):
+            if e + 2 < E:
+                load_w(e + 2)
+            if e == 2:
+                for r, pos in enumerate((pos1, pos2, pos3)):
+                    t = keep.tile([P, T // STRIPE], U16, name=f"pos_sb{r}")
+                    nc.sync.dma_start(t[:], pos)
+                    pos_sb.append(t)
+            if e + 2 == E - 1:
+                gate_sb = raw_pool.tile([P, TOP, T], F32, name="gate_sb", tag="raw")
+                nc.sync.dma_start(gate_sb[:], gate.rearrange("r n t -> n r t"))
+            g = (e + 1) // 2
+            col = (e - GROUPS[g][0]) * C
+            grouped = stage.tile([P, PASSES, N, PACK], BF16, name=f"grouped{e}", tag=f"stage{e}", align_bytes=64)
+            codes = code_pool.tile([P, PASSES * N], U32, name=f"codes{e}", tag="codes", align_bytes=64)
+            plane = code_pool.tile([P, PASSES * N], U8, name=f"plane{e}", tag="plane", align_bytes=64)
+            acc = psum.tile([N, C], F32, name=f"acc{e}", tag="acc")
+            n_pass = PASSES // PIECES[e]
+            for piece in range(PIECES[e]):
+                o0 = piece * n_pass
+                src = raw[e, piece]
+                if n_pass == 1:
+                    half = N // 2
+                    cast(nc.scalar.copy, grouped[:, o0 : o0 + 1, :half, :], src[:, :, :, :half])
+                    cast(nc.vector.tensor_copy, grouped[:, o0 : o0 + 1, half:, :], src[:, :, :, half:])
+                else:
+                    split = n_pass - VEC_PASSES[e]
+                    cast(nc.scalar.copy, grouped[:, o0 : o0 + split], src[:, :split])
+                    if split < n_pass:
+                        cast(nc.vector.tensor_copy, grouped[:, o0 + split : o0 + n_pass], src[:, split:])
+                cols = slice(o0 * N, (o0 + n_pass) * N)
+                nc.vector.quantize_mx(
+                    codes[:, cols].bitcast(FP8X4),
+                    plane[:, cols],
+                    grouped[:, o0 : o0 + n_pass].rearrange("p o n j -> p (o n j)"),
+                )
+                for o in range(o0, o0 + n_pass):
+                    nc.tensor.matmul_mx(
+                        acc[:],
+                        lhsT=codes[:, o * N : (o + 1) * N].bitcast(FP8X4),
+                        lhsT_scale=plane[:, o * N : (o + 1) * N],
+                        rhs=slot_words[g, o // 2][:, o % 2, col : col + C].bitcast(FP8X4),
+                        rhs_scale=slot_scales[g][4 * o : P, col : col + C],
+                        start=(o == 0),
+                        stop=(o == PASSES - 1),
+                    )
+            if e < len(later):
+                gl, hl = later[e]
+                gather_words(gl, hl, f"stage{e}")
+                if hl == 1:
+                    gather_scales(gl)
+            nc.scalar.activation(y[:, e * C : (e + 1) * C], acc[:], GELU, bias=b_sb[:, e : e + 1])
+
+        width = T // 2
+        prod = {}
+
+        def product(r, c):
+            t = keep.tile([P, width], F32, name=f"prod{r}_{c}")
+            lst = pos_sb[r][:, c * width // STRIPE : (c + 1) * width // STRIPE]
+            nc.vector.tensor_tensor(t[:], y[:].indirect(lst), gate_sb[:, r, c * width : (c + 1) * width], MULT)
+            prod[r, c] = t
+
+        part = {}
+        for c in range(2):
+            product(0, c)
+            product(1, c)
+        for c in range(2):
+            part[c] = keep.tile([P, width], F32, name=f"part{c}")
+            nc.vector.tensor_tensor(part[c][:], prod[0, c][:], prod[1, c][:], ADD)
+        for c in range(2):
+            product(2, c)
+        for c in range(2):
+            res = keep.tile([P, width], F32, name=f"res{c}")
+            nc.vector.tensor_tensor(res[:], part[c][:], prod[2, c][:], ADD)
+            nc.sync.dma_start(out[:, c * width : (c + 1) * width], res[:])

@@ -21,10 +21,14 @@ P = 128
 PACK = 4
 PASSES = K // (P * PACK)
 STRIPE = 16
-RUN = 4
-LEAD = 3
-GROUPS = [[0]] + [[e, e + 1] for e in range(1, E, 2)]
-VEC_PASSES = [0,0,0,0,0,0,0,0,0,0,0,0,0,1,0]
+RUN = 2
+GATE_AFTER = 10
+Y_AFTER = 11
+BANKS = [[0,1,2,3],[4,5,6,7],[8,9,10,11],[12,13],[14]]
+GELU_AFTER = {11: range(0, 8), 12: range(8, 12), 14: range(12, 15)}
+GROUP = 5
+WINDOW = 896
+VEC_PASSES = [0,0,1,0,1,0,1,0,1,0,2,2,2,2,0]
 PIECES = [2,1,1,1,1,1,1,1,1,1,1,1,1,1,4]
 
 
@@ -35,13 +39,12 @@ def tile_moe_pkd_lin_gelu_kernel(tc, x_words, x_scales, w, b, gate, offs, pos1, 
         stage = ctx.enter_context(tc.tile_pool(name="stage", bufs=1))
         raw_pool = ctx.enter_context(tc.tile_pool(name="raw", bufs=8))
         code_pool = ctx.enter_context(tc.tile_pool(name="codes", bufs=4))
-        sg_pool = ctx.enter_context(tc.tile_pool(name="sg", bufs=3))
-        psum = ctx.enter_context(tc.psum_pool(name="psum", bufs=4))
+        psum = ctx.enter_context(tc.psum_pool(name="psum", bufs=1))
 
         offs_sb = keep.tile([P, E * C // STRIPE], U16, name="offs_sb")
         nc.sync.dma_start(offs_sb[:], offs)
 
-        x_plane = keep.tile([P, T], U8, name="x_plane", align_bytes=64)
+        x_plane = keep.tile([P, WINDOW], U8, name="x_plane", align_bytes=64)
         nc.vector.memset(x_plane[:].bitcast(I32), 0)
 
         warm = keep.tile([P, 1], F32, name="warm")
@@ -49,52 +52,56 @@ def tile_moe_pkd_lin_gelu_kernel(tc, x_words, x_scales, w, b, gate, offs, pos1, 
         warm_out = keep.tile([P, 1], F32, name="warm_out")
         nc.scalar.activation(warm_out[:], warm[:], GELU)
 
-        words_hbm = x_words.rearrange("o p t r -> p o (t r)").bitcast(I32)
+        words_hbm = x_words.rearrange("o p t r -> o p (t r)").bitcast(I32)
         scales_hbm = x_scales.bitcast(I32)
-        x_half = [keep.tile([P, 2, T], I32, name=f"x_half{h}", align_bytes=64) for h in range(2)]
+        x_pass = [keep.tile([P, WINDOW], I32, name=f"x_pass{o}", align_bytes=64) for o in range(PASSES)]
+        for o in range(PASSES):
+            nc.gpsimd.memset(x_pass[o][:, T:], 0)
         raw = {}
 
-        def load_x(h):
-            nc.sync.dma_start(x_half[h][:], words_hbm[:, 2 * h : 2 * h + 2, :])
+        def load_x(o):
+            nc.sync.dma_start(x_pass[o][:, :T], words_hbm[o])
 
-        def load_w(e):
+        def load_w(e, only=None):
             n_pass = PASSES // PIECES[e]
-            for piece in range(PIECES[e]):
-                t = raw_pool.tile([P, n_pass, PACK, N], F32, name=f"raw{e}_{piece}", tag="raw")
+            for piece in range(PIECES[e]) if only is None else [only]:
+                if e in (GATE_AFTER, Y_AFTER):
+                    t = stage.tile([P, n_pass, PACK, N], F32, name=f"raw{e}_{piece}", tag=f"late{e}")
+                else:
+                    t = raw_pool.tile([P, n_pass, PACK, N], F32, name=f"raw{e}_{piece}", tag="raw")
                 rows = w[e, piece * n_pass * P * PACK : (piece + 1) * n_pass * P * PACK, :]
                 nc.sync.dma_start(t[:], rows.rearrange("(o p j) n -> p o j n", p=P, j=PACK))
                 raw[e, piece] = t
 
         def load_scales():
             for q in range(4):
-                nc.sync.dma_start(x_plane[32 * q : 32 * q + 16, :].bitcast(I32), scales_hbm[:, 4 * q : 4 * q + 4, :])
+                nc.sync.dma_start(x_plane[32 * q : 32 * q + 16, :T].bitcast(I32), scales_hbm[:, 4 * q : 4 * q + 4, :])
 
         load_x(0)
         load_x(1)
-        load_w(0)
+        load_w(0, 0)
+        load_x(2)
+        load_x(3)
+        load_w(0, 1)
         load_scales()
         load_w(1)
         b_sb = keep.tile([P, E], F32, name="b_sb")
         nc.sync.dma_start(b_sb[:], b)
         pos_sb = []
-        y = keep.tile([P, E * C], F32, name="y")
+        banks = [psum.tile([N, len(group) * C], F32, name=f"bank{i}") for i, group in enumerate(BANKS)]
+        sums = {e: banks[i][:, k * C : (k + 1) * C] for i, group in enumerate(BANKS) for k, e in enumerate(group)}
 
-        slot_words = {}
-        slot_scales = {}
+        gathered = {}
 
-        def list_slice(g):
-            return offs_sb[:, GROUPS[g][0] * C // STRIPE : (GROUPS[g][-1] + 1) * C // STRIPE]
-
-        def gather_words(g, h, tag):
-            t = stage.tile([P, 2, len(GROUPS[g]) * C], U32, name=f"xg{g}_{h}", tag=tag, align_bytes=64)
-            for o in range(2):
-                nc.vector.tensor_copy(t[:, o, :], x_half[h][:, o, :].bitcast(U32).indirect(list_slice(g)))
-            slot_words[g, h] = t
-
-        def gather_scales(g):
-            t = sg_pool.tile([P, len(GROUPS[g]) * C], U8, name=f"sg{g}", tag="sg", align_bytes=64)
-            nc.vector.tensor_copy(t[:], x_plane[:].indirect(list_slice(g)))
-            slot_scales[g] = t
+        def gather(g, step, tag):
+            lst = offs_sb[:, g * GROUP * C // STRIPE : (g + 1) * GROUP * C // STRIPE]
+            if step < PASSES:
+                t = stage.tile([P, GROUP * C], U32, name=f"xg{g}_{step}", tag=tag, align_bytes=64)
+                nc.vector.tensor_copy(t[:], x_pass[step][:].bitcast(U32).indirect(lst))
+            else:
+                t = stage.tile([P, GROUP * C], U8, name=f"sg{g}", tag=tag, align_bytes=64)
+                nc.vector.tensor_copy(t[:], x_plane[:].indirect(lst))
+            gathered[g, step] = t
 
         def cast(engine_copy, dst, src):
             engine_copy(
@@ -102,13 +109,8 @@ def tile_moe_pkd_lin_gelu_kernel(tc, x_words, x_scales, w, b, gate, offs, pos1, 
                 src.rearrange("p o j (c i) -> p o c j i", i=RUN),
             )
 
-        first = [g for g in range(len(GROUPS)) if GROUPS[g][0] < LEAD]
-        later = [(g, h) for g in range(len(first), len(GROUPS)) for h in range(2)]
-        for h in range(2):
-            for g in first:
-                gather_words(g, h, f"first{g}_{h}")
-        for g in first:
-            gather_scales(g)
+        for step in range(PASSES + 1):
+            gather(0, step, f"first{step}")
 
         for e in range(E):
             if e + 2 < E:
@@ -118,15 +120,11 @@ def tile_moe_pkd_lin_gelu_kernel(tc, x_words, x_scales, w, b, gate, offs, pos1, 
                     t = keep.tile([P, T // STRIPE], U16, name=f"pos_sb{r}")
                     nc.sync.dma_start(t[:], pos)
                     pos_sb.append(t)
-            if e + 2 == E - 1:
-                gate_sb = raw_pool.tile([P, TOP, T], F32, name="gate_sb", tag="raw")
-                nc.sync.dma_start(gate_sb[:], gate.rearrange("r n t -> n r t"))
-            g = (e + 1) // 2
-            col = (e - GROUPS[g][0]) * C
+            g = e // GROUP
+            col = (e % GROUP) * C
             grouped = stage.tile([P, PASSES, N, PACK], BF16, name=f"grouped{e}", tag=f"stage{e}", align_bytes=64)
             codes = code_pool.tile([P, PASSES * N], U32, name=f"codes{e}", tag="codes", align_bytes=64)
             plane = code_pool.tile([P, PASSES * N], U8, name=f"plane{e}", tag="plane", align_bytes=64)
-            acc = psum.tile([N, C], F32, name=f"acc{e}", tag="acc")
             n_pass = PASSES // PIECES[e]
             for piece in range(PIECES[e]):
                 o0 = piece * n_pass
@@ -148,20 +146,23 @@ def tile_moe_pkd_lin_gelu_kernel(tc, x_words, x_scales, w, b, gate, offs, pos1, 
                 )
                 for o in range(o0, o0 + n_pass):
                     nc.tensor.matmul_mx(
-                        acc[:],
+                        sums[e],
                         lhsT=codes[:, o * N : (o + 1) * N].bitcast(FP8X4),
                         lhsT_scale=plane[:, o * N : (o + 1) * N],
-                        rhs=slot_words[g, o // 2][:, o % 2, col : col + C].bitcast(FP8X4),
-                        rhs_scale=slot_scales[g][4 * o : P, col : col + C],
+                        rhs=gathered[g, o][:, col : col + C].bitcast(FP8X4),
+                        rhs_scale=gathered[g, PASSES][4 * o : P, col : col + C],
                         start=(o == 0),
                         stop=(o == PASSES - 1),
                     )
-            if e < len(later):
-                gl, hl = later[e]
-                gather_words(gl, hl, f"stage{e}")
-                if hl == 1:
-                    gather_scales(gl)
-            nc.scalar.activation(y[:, e * C : (e + 1) * C], acc[:], GELU, bias=b_sb[:, e : e + 1])
+            if e + GROUP < E:
+                gather(g + 1, e % GROUP, f"stage{e}")
+            if e == E - 3:
+                gate_sb = stage.tile([P, TOP, T], F32, name="gate_sb", tag=f"late{GATE_AFTER}")
+                nc.sync.dma_start(gate_sb[:], gate.rearrange("r n t -> n r t"))
+            if e == Y_AFTER:
+                y = stage.tile([P, E * C], F32, name="y", tag=f"late{Y_AFTER}")
+            for done in GELU_AFTER.get(e, []):
+                nc.scalar.activation(y[:, done * C : (done + 1) * C], sums[done], GELU, bias=b_sb[:, done : done + 1])
 
         width = T // 2
         prod = {}

@@ -28,7 +28,7 @@ BANKS = [[0,1,2,3],[4,5,6,7],[8,9,10,11],[12,13],[14]]
 GELU_AFTER = {11: range(0, 8), 12: range(8, 12), 14: range(12, 15)}
 GROUP = 5
 WINDOW = 896
-VEC_PASSES = [0,0,1,0,1,0,1,0,1,0,2,2,2,2,0]
+VEC_PASSES = [0,0,0,0,0,0,0,0,0,0,0,2,4,2,0]
 PIECES = [2,1,1,1,1,1,1,1,1,1,1,1,1,1,4]
 
 
@@ -44,17 +44,12 @@ def tile_moe_pkd_lin_gelu_kernel(tc, x_words, x_scales, w, b, gate, offs, pos1, 
         offs_sb = keep.tile([P, E * C // STRIPE], U16, name="offs_sb")
         nc.sync.dma_start(offs_sb[:], offs)
 
-        x_plane = keep.tile([P, WINDOW], U8, name="x_plane", align_bytes=64)
+        x_plane = keep.tile([P, WINDOW], U8, name="x_plane", align_bytes=256)
         nc.vector.memset(x_plane[:].bitcast(I32), 0)
-
-        warm = keep.tile([P, 1], F32, name="warm")
-        nc.vector.memset(warm[:], 0.0)
-        warm_out = keep.tile([P, 1], F32, name="warm_out")
-        nc.scalar.activation(warm_out[:], warm[:], GELU)
 
         words_hbm = x_words.rearrange("o p t r -> o p (t r)").bitcast(I32)
         scales_hbm = x_scales.bitcast(I32)
-        x_pass = [keep.tile([P, WINDOW], I32, name=f"x_pass{o}", align_bytes=64) for o in range(PASSES)]
+        x_pass = [keep.tile([P, WINDOW], I32, name=f"x_pass{o}", align_bytes=256) for o in range(PASSES)]
         for o in range(PASSES):
             nc.gpsimd.memset(x_pass[o][:, T:], 0)
         raw = {}
@@ -66,9 +61,9 @@ def tile_moe_pkd_lin_gelu_kernel(tc, x_words, x_scales, w, b, gate, offs, pos1, 
             n_pass = PASSES // PIECES[e]
             for piece in range(PIECES[e]) if only is None else [only]:
                 if e in (GATE_AFTER, Y_AFTER):
-                    t = stage.tile([P, n_pass, PACK, N], F32, name=f"raw{e}_{piece}", tag=f"late{e}")
+                    t = stage.tile([P, n_pass, PACK, N], F32, name=f"raw{e}_{piece}", tag=f"late{e}", align_bytes=256)
                 else:
-                    t = raw_pool.tile([P, n_pass, PACK, N], F32, name=f"raw{e}_{piece}", tag="raw")
+                    t = raw_pool.tile([P, n_pass, PACK, N], F32, name=f"raw{e}_{piece}", tag="raw", align_bytes=256)
                 rows = w[e, piece * n_pass * P * PACK : (piece + 1) * n_pass * P * PACK, :]
                 nc.sync.dma_start(t[:], rows.rearrange("(o p j) n -> p o j n", p=P, j=PACK))
                 raw[e, piece] = t
@@ -135,7 +130,8 @@ def tile_moe_pkd_lin_gelu_kernel(tc, x_words, x_scales, w, b, gate, offs, pos1, 
                     cast(nc.vector.tensor_copy, grouped[:, o0 : o0 + 1, half:, :], src[:, :, :, half:])
                 else:
                     split = n_pass - VEC_PASSES[e]
-                    cast(nc.scalar.copy, grouped[:, o0 : o0 + split], src[:, :split])
+                    if split > 0:
+                        cast(nc.scalar.copy, grouped[:, o0 : o0 + split], src[:, :split])
                     if split < n_pass:
                         cast(nc.vector.tensor_copy, grouped[:, o0 + split : o0 + n_pass], src[:, split:])
                 cols = slice(o0 * N, (o0 + n_pass) * N)
@@ -157,10 +153,11 @@ def tile_moe_pkd_lin_gelu_kernel(tc, x_words, x_scales, w, b, gate, offs, pos1, 
             if e + GROUP < E:
                 gather(g + 1, e % GROUP, f"stage{e}")
             if e == E - 3:
-                gate_sb = stage.tile([P, TOP, T], F32, name="gate_sb", tag=f"late{GATE_AFTER}")
-                nc.sync.dma_start(gate_sb[:], gate.rearrange("r n t -> n r t"))
+                gate_sb = stage.tile([P, TOP, T], F32, name="gate_sb", tag=f"late{GATE_AFTER}", align_bytes=256)
+                for r in range(TOP):
+                    nc.sync.dma_start(gate_sb[:, r, :], gate[r])
             if e == Y_AFTER:
-                y = stage.tile([P, E * C], F32, name="y", tag=f"late{Y_AFTER}")
+                y = stage.tile([P, E * C], F32, name="y", tag=f"late{Y_AFTER}", align_bytes=256)
             for done in GELU_AFTER.get(e, []):
                 nc.scalar.activation(y[:, done * C : (done + 1) * C], sums[done], GELU, bias=b_sb[:, done : done + 1])
 
@@ -183,6 +180,6 @@ def tile_moe_pkd_lin_gelu_kernel(tc, x_words, x_scales, w, b, gate, offs, pos1, 
         for c in range(2):
             product(2, c)
         for c in range(2):
-            res = keep.tile([P, width], F32, name=f"res{c}")
+            res = keep.tile([P, width], F32, name=f"res{c}", align_bytes=256)
             nc.vector.tensor_tensor(res[:], part[c][:], prod[2, c][:], ADD)
             nc.sync.dma_start(out[:, c * width : (c + 1) * width], res[:])

@@ -37,7 +37,7 @@ def tile_moe_pkd_lin_gelu_kernel(tc, x_words, x_scales, w, b, gate, offs, pos1, 
     with ExitStack() as ctx:
         keep = ctx.enter_context(tc.tile_pool(name="keep", bufs=1))
         stage = ctx.enter_context(tc.tile_pool(name="stage", bufs=1))
-        raw_pool = ctx.enter_context(tc.tile_pool(name="raw", bufs=8))
+        raw_pool = ctx.enter_context(tc.tile_pool(name="raw", bufs=6))
         code_pool = ctx.enter_context(tc.tile_pool(name="codes", bufs=4))
         psum = ctx.enter_context(tc.psum_pool(name="psum", bufs=1))
 
@@ -60,10 +60,7 @@ def tile_moe_pkd_lin_gelu_kernel(tc, x_words, x_scales, w, b, gate, offs, pos1, 
         def load_w(e, only=None):
             n_pass = PASSES // PIECES[e]
             for piece in range(PIECES[e]) if only is None else [only]:
-                if e in (GATE_AFTER, Y_AFTER):
-                    t = stage.tile([P, n_pass, PACK, N], F32, name=f"raw{e}_{piece}", tag=f"late{e}", align_bytes=256)
-                else:
-                    t = raw_pool.tile([P, n_pass, PACK, N], F32, name=f"raw{e}_{piece}", tag="raw", align_bytes=256)
+                t = stage.tile([P, n_pass, PACK, N], F32, name=f"raw{e}_{piece}", tag=f"raw{e}_{piece}", align_bytes=256)
                 rows = w[e, piece * n_pass * P * PACK : (piece + 1) * n_pass * P * PACK, :]
                 nc.sync.dma_start(t[:], rows.rearrange("(o p j) n -> p o j n", p=P, j=PACK))
                 raw[e, piece] = t
@@ -91,10 +88,10 @@ def tile_moe_pkd_lin_gelu_kernel(tc, x_words, x_scales, w, b, gate, offs, pos1, 
         def gather(g, step, tag):
             lst = offs_sb[:, g * GROUP * C // STRIPE : (g + 1) * GROUP * C // STRIPE]
             if step < PASSES:
-                t = stage.tile([P, GROUP * C], U32, name=f"xg{g}_{step}", tag=tag, align_bytes=64)
+                t = stage.tile([P, GROUP * C], U32, name=f"xg{g}_{step}", tag=tag, align_bytes=256)
                 nc.vector.tensor_copy(t[:], x_pass[step][:].bitcast(U32).indirect(lst))
             else:
-                t = stage.tile([P, GROUP * C], U8, name=f"sg{g}", tag=tag, align_bytes=64)
+                t = stage.tile([P, GROUP * C], U8, name=f"sg{g}", tag=tag, align_bytes=256)
                 nc.vector.tensor_copy(t[:], x_plane[:].indirect(lst))
             gathered[g, step] = t
 
@@ -117,7 +114,7 @@ def tile_moe_pkd_lin_gelu_kernel(tc, x_words, x_scales, w, b, gate, offs, pos1, 
                     pos_sb.append(t)
             g = e // GROUP
             col = (e % GROUP) * C
-            grouped = stage.tile([P, PASSES, N, PACK], BF16, name=f"grouped{e}", tag=f"stage{e}", align_bytes=64)
+            grouped = raw_pool.tile([P, PASSES, N, PACK], BF16, name=f"grouped{e}", tag="grouped", align_bytes=64)
             codes = code_pool.tile([P, PASSES * N], U32, name=f"codes{e}", tag="codes", align_bytes=64)
             plane = code_pool.tile([P, PASSES * N], U8, name=f"plane{e}", tag="plane", align_bytes=64)
             n_pass = PASSES // PIECES[e]
@@ -151,13 +148,13 @@ def tile_moe_pkd_lin_gelu_kernel(tc, x_words, x_scales, w, b, gate, offs, pos1, 
                         stop=(o == PASSES - 1),
                     )
             if e + GROUP < E:
-                gather(g + 1, e % GROUP, f"stage{e}")
+                gather(g + 1, e % GROUP, f"raw{e}_{PIECES[e] - 1}")
             if e == E - 3:
-                gate_sb = stage.tile([P, TOP, T], F32, name="gate_sb", tag=f"late{GATE_AFTER}", align_bytes=256)
+                gate_sb = stage.tile([P, TOP, T], F32, name="gate_sb", tag=f"raw{GATE_AFTER}_0", align_bytes=256)
                 for r in range(TOP):
                     nc.sync.dma_start(gate_sb[:, r, :], gate[r])
             if e == Y_AFTER:
-                y = stage.tile([P, E * C], F32, name="y", tag=f"late{Y_AFTER}", align_bytes=256)
+                y = stage.tile([P, E * C], F32, name="y", tag=f"raw{Y_AFTER}_0", align_bytes=256)
             for done in GELU_AFTER.get(e, []):
                 nc.scalar.activation(y[:, done * C : (done + 1) * C], sums[done], GELU, bias=b_sb[:, done : done + 1])
 

@@ -14,22 +14,22 @@ U16 = mybir.dt.uint16
 U8 = mybir.dt.uint8
 FP8X4 = mybir.dt.float8_e4m3fn_x4
 GELU = mybir.ActivationFunctionType.Gelu_apprx_tanh
+COPY = mybir.ActivationFunctionType.Copy
 MULT = mybir.AluOpType.mult
 ADD = mybir.AluOpType.add
 
 P = 128
 PACK = 4
 PASSES = K // (P * PACK)
+SLOTS = E * C
 STRIPE = 16
 RUN = 2
-GATE_AFTER = 10
-Y_AFTER = 11
-BANKS = [[0,1,2,3],[4,5,6,7],[8,9,10,11],[12,13],[14]]
-GELU_AFTER = {11: range(0, 8), 12: range(8, 12), 14: range(12, 15)}
-GROUP = 5
-WINDOW = 896
-VEC_PASSES = [0,0,0,0,0,0,0,0,0,0,0,2,4,2,0]
-PIECES = [2,1,1,1,1,1,1,1,1,1,1,1,1,1,4]
+WINDOW = 2 * T
+CUT = SLOTS // 2
+LAST = E - 1
+SCALAR_ONLY = 12
+FIRST_TOKENS = 384
+BANK_OF = [0, 0, 0, 1, 1, 1, 2, 2, 2, 3, 3, 3, 4, 5, 6]
 
 
 def tile_moe_pkd_lin_gelu_kernel(tc, x_words, x_scales, w, b, gate, offs, pos1, pos2, pos3, out):
@@ -37,63 +37,72 @@ def tile_moe_pkd_lin_gelu_kernel(tc, x_words, x_scales, w, b, gate, offs, pos1, 
     with ExitStack() as ctx:
         keep = ctx.enter_context(tc.tile_pool(name="keep", bufs=1))
         stage = ctx.enter_context(tc.tile_pool(name="stage", bufs=1))
-        raw_pool = ctx.enter_context(tc.tile_pool(name="raw", bufs=6))
-        code_pool = ctx.enter_context(tc.tile_pool(name="codes", bufs=4))
         psum = ctx.enter_context(tc.psum_pool(name="psum", bufs=1))
 
-        offs_sb = keep.tile([P, E * C // STRIPE], U16, name="offs_sb")
+        offs_sb = keep.tile([P, SLOTS // STRIPE], U16, name="offs_sb")
         nc.sync.dma_start(offs_sb[:], offs)
 
         x_plane = keep.tile([P, WINDOW], U8, name="x_plane", align_bytes=256)
         nc.vector.memset(x_plane[:].bitcast(I32), 0)
+        x_all = keep.tile([P, (PASSES + 1) * T], I32, name="x_all", align_bytes=256)
+        nc.vector.memset(x_all[:, PASSES * T :], 0)
 
         words_hbm = x_words.rearrange("o p t r -> o p (t r)").bitcast(I32)
         scales_hbm = x_scales.bitcast(I32)
-        x_pass = [keep.tile([P, WINDOW], I32, name=f"x_pass{o}", align_bytes=256) for o in range(PASSES)]
-        for o in range(PASSES):
-            nc.gpsimd.memset(x_pass[o][:, T:], 0)
+
+        def pieces(e):
+            return PASSES if e == LAST else 2 if e in (0, LAST - 1) else 1
+
         raw = {}
 
         def load_x(o):
-            nc.sync.dma_start(x_pass[o][:, :T], words_hbm[o])
+            at = (PASSES - 1 - o) * T
+            nc.sync.dma_start(x_all[:, at : at + T], words_hbm[o])
 
-        def load_w(e, only=None):
-            n_pass = PASSES // PIECES[e]
-            for piece in range(PIECES[e]) if only is None else [only]:
+        def load_w(e):
+            n_pass = PASSES // pieces(e)
+            for piece in range(pieces(e)):
                 t = stage.tile([P, n_pass, PACK, N], F32, name=f"raw{e}_{piece}", tag=f"raw{e}_{piece}", align_bytes=256)
                 rows = w[e, piece * n_pass * P * PACK : (piece + 1) * n_pass * P * PACK, :]
                 nc.sync.dma_start(t[:], rows.rearrange("(o p j) n -> p o j n", p=P, j=PACK))
                 raw[e, piece] = t
 
-        def load_scales():
-            for q in range(4):
-                nc.sync.dma_start(x_plane[32 * q : 32 * q + 16, :T].bitcast(I32), scales_hbm[:, 4 * q : 4 * q + 4, :])
-
-        load_x(0)
-        load_x(1)
-        load_w(0, 0)
-        load_x(2)
-        load_x(3)
-        load_w(0, 1)
-        load_scales()
-        load_w(1)
         b_sb = keep.tile([P, E], F32, name="b_sb")
-        nc.sync.dma_start(b_sb[:], b)
+        for e in range(E):
+            if e in (0, 1, 3, 5):
+                load_x((e + 1) // 2)
+            if e == 5:
+                for q in range(4):
+                    nc.sync.dma_start(x_plane[32 * q : 32 * q + 16, :T].bitcast(I32), scales_hbm[:, 4 * q : 4 * q + 4, :])
+            if e == 7:
+                nc.sync.dma_start(b_sb[:], b)
+            load_w(e)
         pos_sb = []
-        banks = [psum.tile([N, len(group) * C], F32, name=f"bank{i}") for i, group in enumerate(BANKS)]
-        sums = {e: banks[i][:, k * C : (k + 1) * C] for i, group in enumerate(BANKS) for k, e in enumerate(group)}
+        for r, pos in enumerate((pos1, pos2, pos3)):
+            t = keep.tile([P, T // STRIPE], U16, name=f"pos_sb{r}")
+            nc.sync.dma_start(t[:], pos)
+            pos_sb.append(t)
+        gate_sb = []
+        for r in range(TOP):
+            t = keep.tile([P, T], F32, name=f"gate_sb{r}", align_bytes=256)
+            nc.sync.dma_start(t[:], gate[r])
+            gate_sb.append(t)
 
-        gathered = {}
+        slot_words = []
+        for o in range(PASSES):
+            t = keep.tile([P, SLOTS], U32, name=f"slot_words{o}", align_bytes=256)
+            at = (PASSES - 1 - o) * T
+            for s0 in range(0, SLOTS, CUT):
+                lst = offs_sb[:, s0 // STRIPE : (s0 + CUT) // STRIPE]
+                nc.vector.tensor_copy(t[:, s0 : s0 + CUT], x_all[:, at : at + WINDOW].bitcast(U32).indirect(lst))
+            slot_words.append(t)
+        slot_plane = keep.tile([P, SLOTS], U8, name="slot_plane", align_bytes=256)
+        for s0 in range(0, SLOTS, CUT):
+            lst = offs_sb[:, s0 // STRIPE : (s0 + CUT) // STRIPE]
+            nc.vector.tensor_copy(slot_plane[:, s0 : s0 + CUT], x_plane[:].indirect(lst))
 
-        def gather(g, step, tag):
-            lst = offs_sb[:, g * GROUP * C // STRIPE : (g + 1) * GROUP * C // STRIPE]
-            if step < PASSES:
-                t = stage.tile([P, GROUP * C], U32, name=f"xg{g}_{step}", tag=tag, align_bytes=256)
-                nc.vector.tensor_copy(t[:], x_pass[step][:].bitcast(U32).indirect(lst))
-            else:
-                t = stage.tile([P, GROUP * C], U8, name=f"sg{g}", tag=tag, align_bytes=256)
-                nc.vector.tensor_copy(t[:], x_plane[:].indirect(lst))
-            gathered[g, step] = t
+        banks = [psum.tile([N, BANK_OF.count(i) * C], F32, name=f"bank{i}") for i in range(max(BANK_OF) + 1)]
+        sums = [banks[BANK_OF[e]][:, (e - BANK_OF.index(BANK_OF[e])) * C : (e - BANK_OF.index(BANK_OF[e]) + 1) * C] for e in range(E)]
 
         def cast(engine_copy, dst, src):
             engine_copy(
@@ -101,82 +110,103 @@ def tile_moe_pkd_lin_gelu_kernel(tc, x_words, x_scales, w, b, gate, offs, pos1, 
                 src.rearrange("p o j (c i) -> p o c j i", i=RUN),
             )
 
-        for step in range(PASSES + 1):
-            gather(0, step, f"first{step}")
+        def quantize_and_multiply(e, grouped, codes, plane, o0, n_pass):
+            cols = slice(o0 * N, (o0 + n_pass) * N)
+            nc.vector.quantize_mx(
+                codes[:, cols].bitcast(FP8X4),
+                plane[:, cols],
+                grouped[:, o0 : o0 + n_pass].rearrange("p o n j -> p (o n j)"),
+            )
+            for o in range(o0, o0 + n_pass):
+                nc.tensor.matmul_mx(
+                    sums[e],
+                    lhsT=codes[:, o * N : (o + 1) * N].bitcast(FP8X4),
+                    lhsT_scale=plane[:, o * N : (o + 1) * N],
+                    rhs=slot_words[o][:, e * C : (e + 1) * C].bitcast(FP8X4),
+                    rhs_scale=slot_plane[4 * o : P, e * C : (e + 1) * C],
+                    start=(o == 0),
+                    stop=(o == PASSES - 1),
+                )
+
+        def gelu(e):
+            nc.scalar.activation(y[:, e * C : (e + 1) * C], sums[e], GELU, bias=b_sb[:, e : e + 1])
 
         for e in range(E):
-            if e + 2 < E:
-                load_w(e + 2)
-            if e == 2:
-                for r, pos in enumerate((pos1, pos2, pos3)):
-                    t = keep.tile([P, T // STRIPE], U16, name=f"pos_sb{r}")
-                    nc.sync.dma_start(t[:], pos)
-                    pos_sb.append(t)
-            g = e // GROUP
-            col = (e % GROUP) * C
-            grouped = raw_pool.tile([P, PASSES, N, PACK], BF16, name=f"grouped{e}", tag="grouped", align_bytes=64)
-            codes = code_pool.tile([P, PASSES * N], U32, name=f"codes{e}", tag="codes", align_bytes=64)
-            plane = code_pool.tile([P, PASSES * N], U8, name=f"plane{e}", tag="plane", align_bytes=64)
-            n_pass = PASSES // PIECES[e]
-            for piece in range(PIECES[e]):
-                o0 = piece * n_pass
-                src = raw[e, piece]
-                if n_pass == 1:
-                    half = N // 2
-                    cast(nc.scalar.copy, grouped[:, o0 : o0 + 1, :half, :], src[:, :, :, :half])
-                    cast(nc.vector.tensor_copy, grouped[:, o0 : o0 + 1, half:, :], src[:, :, :, half:])
-                else:
-                    split = n_pass - VEC_PASSES[e]
-                    if split > 0:
-                        cast(nc.scalar.copy, grouped[:, o0 : o0 + split], src[:, :split])
-                    if split < n_pass:
-                        cast(nc.vector.tensor_copy, grouped[:, o0 + split : o0 + n_pass], src[:, split:])
-                cols = slice(o0 * N, (o0 + n_pass) * N)
-                nc.vector.quantize_mx(
-                    codes[:, cols].bitcast(FP8X4),
-                    plane[:, cols],
-                    grouped[:, o0 : o0 + n_pass].rearrange("p o n j -> p (o n j)"),
-                )
-                for o in range(o0, o0 + n_pass):
-                    nc.tensor.matmul_mx(
-                        sums[e],
-                        lhsT=codes[:, o * N : (o + 1) * N].bitcast(FP8X4),
-                        lhsT_scale=plane[:, o * N : (o + 1) * N],
-                        rhs=gathered[g, o][:, col : col + C].bitcast(FP8X4),
-                        rhs_scale=gathered[g, PASSES][4 * o : P, col : col + C],
-                        start=(o == 0),
-                        stop=(o == PASSES - 1),
-                    )
-            if e + GROUP < E:
-                gather(g + 1, e % GROUP, f"raw{e}_{PIECES[e] - 1}")
-            if e == E - 3:
-                gate_sb = stage.tile([P, TOP, T], F32, name="gate_sb", tag=f"raw{GATE_AFTER}_0", align_bytes=256)
-                for r in range(TOP):
-                    nc.sync.dma_start(gate_sb[:, r, :], gate[r])
-            if e == Y_AFTER:
-                y = stage.tile([P, E * C], F32, name="y", tag=f"raw{Y_AFTER}_0", align_bytes=256)
-            for done in GELU_AFTER.get(e, []):
-                nc.scalar.activation(y[:, done * C : (done + 1) * C], sums[done], GELU, bias=b_sb[:, done : done + 1])
+            reuse = e - 2
+            tag = f"raw{reuse}_0" if 1 <= reuse < SCALAR_ONLY - 1 else f"grouped{e % 3}"
+            grouped = stage.tile([P, PASSES, N, PACK], BF16, name=f"grouped{e}", tag=tag, align_bytes=256)
+            codes = keep.tile([P, PASSES * N], U32, name=f"codes{e}", align_bytes=64)
+            plane = keep.tile([P, PASSES * N], U8, name=f"plane{e}", align_bytes=64)
+            if e < SCALAR_ONLY:
+                n_pass = PASSES // pieces(e)
+                for piece in range(pieces(e)):
+                    cast(nc.scalar.copy, grouped[:, piece * n_pass : (piece + 1) * n_pass], raw[e, piece][:])
+                quantize_and_multiply(e, grouped, codes, plane, 0, PASSES)
+            elif e == SCALAR_ONLY:
+                y = stage.tile([P, SLOTS], F32, name="y", tag=f"raw{e - 1}_0", align_bytes=256)
+                for done in range(e):
+                    gelu(done)
+                for o0 in (0, 2):
+                    cast(nc.vector.tensor_copy, grouped[:, o0 : o0 + 2], raw[e, 0][:, o0 : o0 + 2])
+                for o0 in (0, 2):
+                    quantize_and_multiply(e, grouped, codes, plane, o0, 2)
+            elif e < LAST:
+                cast(nc.vector.tensor_copy, grouped[:, :2], raw[e, 0][:])
+                cast(nc.scalar.copy, grouped[:, 2:], raw[e, 1][:])
+                gelu(e - 1)
+                for o0 in (0, 2):
+                    quantize_and_multiply(e, grouped, codes, plane, o0, 2)
+            else:
+                half = N // 2
+                for o in range(PASSES):
+                    cast(nc.scalar.copy, grouped[:, o : o + 1, :half, :], raw[e, o][:, :, :, :half])
+                    cast(nc.vector.tensor_copy, grouped[:, o : o + 1, half:, :], raw[e, o][:, :, :, half:])
+                    quantize_and_multiply(e, grouped, codes, plane, o, 1)
+                    if o == 1:
+                        gelu(e - 1)
+                gelu(e)
 
-        width = T // 2
-        prod = {}
+        spans = [(0, FIRST_TOKENS), (FIRST_TOKENS, T)]
+        work = {}
+
+        def scratch(label, c):
+            t0, t1 = spans[c]
+            t = stage.tile([P, t1 - t0], F32, name=f"{label}{c}", tag=f"raw{1 + len(work) % 9}_0", align_bytes=256)
+            work[label, c] = t
+            return t
+
+        def looked_up(r, c):
+            t0, t1 = spans[c]
+            return y[:].indirect(pos_sb[r][:, t0 // STRIPE : t1 // STRIPE])
+
+        def weight(r, c):
+            t0, t1 = spans[c]
+            return gate_sb[r][:, t0:t1]
+
+        def fetch(r, c):
+            nc.scalar.activation(scratch(f"got{r}", c)[:], looked_up(r, c), COPY)
 
         def product(r, c):
-            t = keep.tile([P, width], F32, name=f"prod{r}_{c}")
-            lst = pos_sb[r][:, c * width // STRIPE : (c + 1) * width // STRIPE]
-            nc.vector.tensor_tensor(t[:], y[:].indirect(lst), gate_sb[:, r, c * width : (c + 1) * width], MULT)
-            prod[r, c] = t
+            src = looked_up(r, c) if r == 0 else work[f"got{r}", c][:]
+            t = keep.tile([P, spans[c][1] - spans[c][0]], F32, name=f"prod{r}_{c}")
+            nc.vector.tensor_tensor(t[:], src, weight(r, c), MULT)
+            work[f"prod{r}", c] = t
 
-        part = {}
+        def add(label, left, right, c):
+            nc.vector.tensor_tensor(scratch(label, c)[:], work[left, c][:], work[right, c][:], ADD)
+
         for c in range(2):
-            product(0, c)
-            product(1, c)
-        for c in range(2):
-            part[c] = keep.tile([P, width], F32, name=f"part{c}")
-            nc.vector.tensor_tensor(part[c][:], prod[0, c][:], prod[1, c][:], ADD)
-        for c in range(2):
-            product(2, c)
-        for c in range(2):
-            res = keep.tile([P, width], F32, name=f"res{c}", align_bytes=256)
-            nc.vector.tensor_tensor(res[:], part[c][:], prod[2, c][:], ADD)
-            nc.sync.dma_start(out[:, c * width : (c + 1) * width], res[:])
+            fetch(1, c)
+            fetch(2, c)
+        product(0, 0)
+        product(0, 1)
+        product(1, 0)
+        product(2, 0)
+        add("part", "prod0", "prod1", 0)
+        product(1, 1)
+        add("res", "part", "prod2", 0)
+        nc.sync.dma_start(out[:, :FIRST_TOKENS], work["res", 0][:])
+        add("part", "prod0", "prod1", 1)
+        product(2, 1)
+        add("res", "part", "prod2", 1)
+        nc.sync.dma_start(out[:, FIRST_TOKENS:], work["res", 1][:])

@@ -47,6 +47,10 @@ def tile_moe_pkd_lin_gelu_kernel(tc, x_words, x_scales, w, b, gate, offs, pos1, 
         x_all = keep.tile([P, (PASSES + 1) * T], I32, name="x_all", align_bytes=256)
         nc.vector.memset(x_all[:, PASSES * T :], 0)
 
+        warm = keep.tile([P, 16], F32, name="warm")
+        nc.gpsimd.memset(warm[:, :8], 0.0)
+        nc.scalar.activation(warm[:, 8:], warm[:, :8], GELU)
+
         words_hbm = x_words.rearrange("o p t r -> o p (t r)").bitcast(I32)
         scales_hbm = x_scales.bitcast(I32)
 

@@ -27,9 +27,9 @@ RUN = 2
 WINDOW = 2 * T
 CUT = SLOTS // 2
 LAST = E - 1
-SCALAR_ONLY = 12
+HELD = 9
 FIRST_TOKENS = 384
-BANK_OF = [0, 0, 0, 1, 1, 1, 2, 2, 2, 3, 3, 3, 4, 5, 6]
+BANK_OF = [0, 0, 0, 1, 1, 1, 2, 2, 2, 3, 3, 3, 4, 4, 5]
 
 
 def tile_moe_pkd_lin_gelu_kernel(tc, x_words, x_scales, w, b, gate, offs, pos1, pos2, pos3, out):
@@ -86,11 +86,9 @@ def tile_moe_pkd_lin_gelu_kernel(tc, x_words, x_scales, w, b, gate, offs, pos1, 
             t = keep.tile([P, T // STRIPE], U16, name=f"pos_sb{r}")
             nc.sync.dma_start(t[:], pos)
             pos_sb.append(t)
-        gate_sb = []
+        gate_sb = [keep.tile([P, T], F32, name=f"gate_sb{r}", align_bytes=256) for r in range(TOP)]
         for r in range(TOP):
-            t = keep.tile([P, T], F32, name=f"gate_sb{r}", align_bytes=256)
-            nc.sync.dma_start(t[:], gate[r])
-            gate_sb.append(t)
+            nc.sync.dma_start(gate_sb[r][:], gate[r])
 
         slot_words = []
         for o in range(PASSES):
@@ -137,28 +135,35 @@ def tile_moe_pkd_lin_gelu_kernel(tc, x_words, x_scales, w, b, gate, offs, pos1, 
 
         for e in range(E):
             reuse = e - 2
-            tag = f"raw{reuse}_0" if 1 <= reuse < SCALAR_ONLY - 1 else f"grouped{e % 3}"
+            tag = f"raw{reuse}_0" if 1 <= reuse < HELD else f"grouped{e % 3}"
             grouped = stage.tile([P, PASSES, N, PACK], BF16, name=f"grouped{e}", tag=tag, align_bytes=256)
             codes = keep.tile([P, PASSES * N], U32, name=f"codes{e}", align_bytes=64)
             plane = keep.tile([P, PASSES * N], U8, name=f"plane{e}", align_bytes=64)
-            if e < SCALAR_ONLY:
+            if e <= HELD or e == HELD + 2:
                 n_pass = PASSES // pieces(e)
                 for piece in range(pieces(e)):
                     cast(nc.scalar.copy, grouped[:, piece * n_pass : (piece + 1) * n_pass], raw[e, piece][:])
                 quantize_and_multiply(e, grouped, codes, plane, 0, PASSES)
-            elif e == SCALAR_ONLY:
-                y = stage.tile([P, SLOTS], F32, name="y", tag=f"raw{e - 1}_0", align_bytes=256)
-                for done in range(e):
-                    gelu(done)
+                if e == HELD:
+                    y = stage.tile([P, SLOTS], F32, name="y", tag=f"raw{e}_0", align_bytes=256)
+                    for done in range(e):
+                        gelu(done)
+            elif e == HELD + 1:
                 for o0 in (0, 2):
                     cast(nc.vector.tensor_copy, grouped[:, o0 : o0 + 2], raw[e, 0][:, o0 : o0 + 2])
                 for o0 in (0, 2):
                     quantize_and_multiply(e, grouped, codes, plane, o0, 2)
+            elif e < LAST - 1:
+                cast(nc.vector.tensor_copy, grouped[:, :2], raw[e, 0][:, :2])
+                cast(nc.scalar.copy, grouped[:, 2:], raw[e, 0][:, 2:])
+                for done in range(HELD, e):
+                    gelu(done)
+                quantize_and_multiply(e, grouped, codes, plane, 0, PASSES)
             elif e < LAST:
-                cast(nc.vector.tensor_copy, grouped[:, :2], raw[e, 0][:])
-                cast(nc.scalar.copy, grouped[:, 2:], raw[e, 1][:])
-                gelu(e - 1)
-                for o0 in (0, 2):
+                for piece in range(2):
+                    o0 = 2 * piece
+                    cast(nc.vector.tensor_copy, grouped[:, o0 : o0 + 1], raw[e, piece][:, :1])
+                    cast(nc.scalar.copy, grouped[:, o0 + 1 : o0 + 2], raw[e, piece][:, 1:])
                     quantize_and_multiply(e, grouped, codes, plane, o0, 2)
             else:
                 half = N // 2
@@ -167,50 +172,44 @@ def tile_moe_pkd_lin_gelu_kernel(tc, x_words, x_scales, w, b, gate, offs, pos1, 
                     cast(nc.vector.tensor_copy, grouped[:, o : o + 1, half:, :], raw[e, o][:, :, :, half:])
                     quantize_and_multiply(e, grouped, codes, plane, o, 1)
                     if o == 1:
+                        gelu(e - 2)
                         gelu(e - 1)
                 gelu(e)
 
-        spans = [(0, FIRST_TOKENS), (FIRST_TOKENS, T)]
-        work = {}
+        first, second, every = slice(0, FIRST_TOKENS), slice(FIRST_TOKENS, T), slice(0, T)
+        free_tags = [f"raw{e}_0" for e in range(1, HELD)]
 
-        def scratch(label, c):
-            t0, t1 = spans[c]
-            t = stage.tile([P, t1 - t0], F32, name=f"{label}{c}", tag=f"raw{1 + len(work) % 9}_0", align_bytes=256)
-            work[label, c] = t
-            return t
+        def scratch(name, span):
+            tag = free_tags.pop() if free_tags else name
+            return stage.tile([P, span.stop - span.start], F32, name=name, tag=tag, align_bytes=256)
 
-        def looked_up(r, c):
-            t0, t1 = spans[c]
-            return y[:].indirect(pos_sb[r][:, t0 // STRIPE : t1 // STRIPE])
+        def looked_up(r, span):
+            return y[:].indirect(pos_sb[r][:, span.start // STRIPE : span.stop // STRIPE])
 
-        def weight(r, c):
-            t0, t1 = spans[c]
-            return gate_sb[r][:, t0:t1]
+        def fetch(name, r, span):
+            t = scratch(name, span)
+            nc.scalar.activation(t[:], looked_up(r, span), COPY)
+            return t[:]
 
-        def fetch(r, c):
-            nc.scalar.activation(scratch(f"got{r}", c)[:], looked_up(r, c), COPY)
+        def product(name, src, r, span):
+            t = scratch(name, span)
+            nc.vector.tensor_tensor(t[:], src, gate_sb[r][:, span], MULT)
+            return t[:]
 
-        def product(r, c):
-            src = looked_up(r, c) if r == 0 else work[f"got{r}", c][:]
-            t = keep.tile([P, spans[c][1] - spans[c][0]], F32, name=f"prod{r}_{c}")
-            nc.vector.tensor_tensor(t[:], src, weight(r, c), MULT)
-            work[f"prod{r}", c] = t
+        def add(name, left, right, span):
+            t = scratch(name, span)
+            nc.vector.tensor_tensor(t[:], left, right, ADD)
+            return t[:]
 
-        def add(label, left, right, c):
-            nc.vector.tensor_tensor(scratch(label, c)[:], work[left, c][:], work[right, c][:], ADD)
-
-        for c in range(2):
-            fetch(1, c)
-            fetch(2, c)
-        product(0, 0)
-        product(0, 1)
-        product(1, 0)
-        product(2, 0)
-        add("part", "prod0", "prod1", 0)
-        product(1, 1)
-        add("res", "part", "prod2", 0)
-        nc.sync.dma_start(out[:, :FIRST_TOKENS], work["res", 0][:])
-        add("part", "prod0", "prod1", 1)
-        product(2, 1)
-        add("res", "part", "prod2", 1)
-        nc.sync.dma_start(out[:, FIRST_TOKENS:], work["res", 1][:])
+        got1_first = fetch("got1_first", 1, first)
+        got2_first = fetch("got2_first", 2, first)
+        got2_second = fetch("got2_second", 2, second)
+        prod0 = product("prod0", looked_up(0, every), 0, every)
+        prod1_second = product("prod1_second", looked_up(1, second), 1, second)
+        prod1_first = product("prod1_first", got1_first, 1, first)
+        part_second = add("part_second", prod0[:, second], prod1_second, second)
+        part_first = add("part_first", prod0[:, first], prod1_first, first)
+        prod2_first = product("prod2_first", got2_first, 2, first)
+        prod2_second = product("prod2_second", got2_second, 2, second)
+        nc.sync.dma_start(out[:, first], add("res_first", part_first, prod2_first, first))
+        nc.sync.dma_start(out[:, second], add("res_second", part_second, prod2_second, second))

@@ -27,7 +27,9 @@ RUN = 2
 WINDOW = 2 * T
 CUT = SLOTS // 2
 LAST = E - 1
-HELD = 9
+HELD = 10
+LATE = 12
+ON_VECTOR = (11, 13)
 FIRST_TOKENS = 384
 BANK_OF = [0, 0, 0, 1, 1, 1, 2, 2, 2, 3, 3, 3, 4, 4, 5]
 
@@ -71,7 +73,8 @@ def tile_moe_pkd_lin_gelu_kernel(tc, x_words, x_scales, w, b, gate, offs, pos1, 
                 nc.sync.dma_start(t[:], rows.rearrange("(o p j) n -> p o j n", p=P, j=PACK))
                 raw[e, piece] = t
 
-        b_sb = keep.tile([P, E], F32, name="b_sb")
+        b_sb = keep.tile([P, LATE], F32, name="b_sb")
+        b_late = keep.tile([P, E - LATE], F32, name="b_late")
         for e in range(E):
             if e in (0, 1, 3, 5):
                 load_x((e + 1) // 2)
@@ -79,8 +82,9 @@ def tile_moe_pkd_lin_gelu_kernel(tc, x_words, x_scales, w, b, gate, offs, pos1, 
                 for q in range(4):
                     nc.sync.dma_start(x_plane[32 * q : 32 * q + 16, :T].bitcast(I32), scales_hbm[:, 4 * q : 4 * q + 4, :])
             if e == 7:
-                nc.sync.dma_start(b_sb[:], b)
+                nc.sync.dma_start(b_sb[:], b[:, :LATE])
             load_w(e)
+        nc.sync.dma_start(b_late[:], b[:, LATE:])
         pos_sb = []
         for r, pos in enumerate((pos1, pos2, pos3)):
             t = keep.tile([P, T // STRIPE], U16, name=f"pos_sb{r}")
@@ -131,7 +135,8 @@ def tile_moe_pkd_lin_gelu_kernel(tc, x_words, x_scales, w, b, gate, offs, pos1, 
                 )
 
         def gelu(e):
-            nc.scalar.activation(y[:, e * C : (e + 1) * C], sums[e], GELU, bias=b_sb[:, e : e + 1])
+            bias = b_sb[:, e : e + 1] if e < LATE else b_late[:, e - LATE : e - LATE + 1]
+            nc.scalar.activation(y[:, e * C : (e + 1) * C], sums[e], GELU, bias=bias)
 
         for e in range(E):
             reuse = e - 2
@@ -139,42 +144,33 @@ def tile_moe_pkd_lin_gelu_kernel(tc, x_words, x_scales, w, b, gate, offs, pos1, 
             grouped = stage.tile([P, PASSES, N, PACK], BF16, name=f"grouped{e}", tag=tag, align_bytes=256)
             codes = keep.tile([P, PASSES * N], U32, name=f"codes{e}", align_bytes=64)
             plane = keep.tile([P, PASSES * N], U8, name=f"plane{e}", align_bytes=64)
-            if e <= HELD or e == HELD + 2:
-                n_pass = PASSES // pieces(e)
-                for piece in range(pieces(e)):
-                    cast(nc.scalar.copy, grouped[:, piece * n_pass : (piece + 1) * n_pass], raw[e, piece][:])
+            n_pass = PASSES // pieces(e)
+            if e < LAST:
+                engine_copy = nc.vector.tensor_copy if e in ON_VECTOR else nc.scalar.copy
+                if e == LATE:
+                    cast(nc.scalar.copy, grouped[:, 1:], raw[e, 0][:, 1:])
+                    cast(nc.vector.tensor_copy, grouped[:, :1], raw[e, 0][:, :1])
+                else:
+                    for piece in range(pieces(e)):
+                        cast(engine_copy, grouped[:, piece * n_pass : (piece + 1) * n_pass], raw[e, piece][:])
                 quantize_and_multiply(e, grouped, codes, plane, 0, PASSES)
                 if e == HELD:
                     y = stage.tile([P, SLOTS], F32, name="y", tag=f"raw{e}_0", align_bytes=256)
-                    for done in range(e):
+                    for done in range(9):
                         gelu(done)
-            elif e == HELD + 1:
-                for o0 in (0, 2):
-                    cast(nc.vector.tensor_copy, grouped[:, o0 : o0 + 2], raw[e, 0][:, o0 : o0 + 2])
-                for o0 in (0, 2):
-                    quantize_and_multiply(e, grouped, codes, plane, o0, 2)
-            elif e < LAST - 1:
-                cast(nc.vector.tensor_copy, grouped[:, :2], raw[e, 0][:, :2])
-                cast(nc.scalar.copy, grouped[:, 2:], raw[e, 0][:, 2:])
-                for done in range(HELD, e):
-                    gelu(done)
-                quantize_and_multiply(e, grouped, codes, plane, 0, PASSES)
-            elif e < LAST:
-                for piece in range(2):
-                    o0 = 2 * piece
-                    cast(nc.vector.tensor_copy, grouped[:, o0 : o0 + 1], raw[e, piece][:, :1])
-                    cast(nc.scalar.copy, grouped[:, o0 + 1 : o0 + 2], raw[e, piece][:, 1:])
-                    quantize_and_multiply(e, grouped, codes, plane, o0, 2)
+                if e == 12:
+                    for done in range(9, 12):
+                        gelu(done)
             else:
-                half = N // 2
-                for o in range(PASSES):
-                    cast(nc.scalar.copy, grouped[:, o : o + 1, :half, :], raw[e, o][:, :, :, :half])
-                    cast(nc.vector.tensor_copy, grouped[:, o : o + 1, half:, :], raw[e, o][:, :, :, half:])
+                for o in range(PASSES - 1):
+                    cast(nc.scalar.copy, grouped[:, o : o + 1], raw[e, o][:])
                     quantize_and_multiply(e, grouped, codes, plane, o, 1)
-                    if o == 1:
-                        gelu(e - 2)
-                        gelu(e - 1)
-                gelu(e)
+                o, half = PASSES - 1, N // 2
+                cast(nc.scalar.copy, grouped[:, o:, :half, :], raw[e, o][:, :, :, :half])
+                cast(nc.vector.tensor_copy, grouped[:, o:, half:, :], raw[e, o][:, :, :, half:])
+                quantize_and_multiply(e, grouped, codes, plane, o, 1)
+                for done in range(12, E):
+                    gelu(done)
 
         first, second, every = slice(0, FIRST_TOKENS), slice(FIRST_TOKENS, T), slice(0, T)
         free_tags = [f"raw{e}_0" for e in range(1, HELD)]

@@ -27,11 +27,18 @@ RUN = 2
 WINDOW = 2 * T
 CUT = SLOTS // 2
 LAST = E - 1
-HELD = 10
-LATE = 12
-ON_VECTOR = (11, 13)
+SHARES = {
+    10: [(False, 0, 2), (False, 2, 4)],
+    11: [(False, 0, 2), (False, 2, 4)],
+    12: [(True, 0, 4)],
+    13: [(False, 0, 2), (True, 2, 4)],
+}
+X_BEFORE = {0: (3, 4), 3: (2, 3), 5: (0, 2)}
+HALVED = (5, 6, 7, 8, 9, 10, 11, 13)
+PAIRED = 10
+GELUS_BEHIND = {11: range(0, 12), 14: range(12, 15)}
 FIRST_TOKENS = 384
-BANK_OF = [0, 0, 0, 1, 1, 1, 2, 2, 2, 3, 3, 3, 4, 4, 5]
+BANK_OF = [0, 0, 0, 0, 1, 1, 1, 1, 2, 2, 2, 2, 3, 3, 4]
 
 
 def tile_moe_pkd_lin_gelu_kernel(tc, x_words, x_scales, w, b, gate, offs, pos1, pos2, pos3, out):
@@ -57,13 +64,13 @@ def tile_moe_pkd_lin_gelu_kernel(tc, x_words, x_scales, w, b, gate, offs, pos1, 
         scales_hbm = x_scales.bitcast(I32)
 
         def pieces(e):
-            return PASSES if e == LAST else 2 if e in (0, LAST - 1) else 1
+            return PASSES if e == LAST else 2 if e in HALVED else 1
 
         raw = {}
 
-        def load_x(o):
-            at = (PASSES - 1 - o) * T
-            nc.sync.dma_start(x_all[:, at : at + T], words_hbm[o])
+        def load_x(o0, o1):
+            dst = x_all[:, o0 * T : o1 * T].rearrange("p (o t) -> p o t", t=T)
+            nc.sync.dma_start(dst, words_hbm[o0:o1].rearrange("o p t -> p o t"))
 
         def load_w(e):
             n_pass = PASSES // pieces(e)
@@ -73,18 +80,20 @@ def tile_moe_pkd_lin_gelu_kernel(tc, x_words, x_scales, w, b, gate, offs, pos1, 
                 nc.sync.dma_start(t[:], rows.rearrange("(o p j) n -> p o j n", p=P, j=PACK))
                 raw[e, piece] = t
 
-        b_sb = keep.tile([P, LATE], F32, name="b_sb")
-        b_late = keep.tile([P, E - LATE], F32, name="b_late")
+        bias = {}
         for e in range(E):
-            if e in (0, 1, 3, 5):
-                load_x((e + 1) // 2)
-            if e == 5:
+            if e in X_BEFORE:
+                load_x(*X_BEFORE[e])
+            if e == 1:
                 for q in range(4):
                     nc.sync.dma_start(x_plane[32 * q : 32 * q + 16, :T].bitcast(I32), scales_hbm[:, 4 * q : 4 * q + 4, :])
-            if e == 7:
-                nc.sync.dma_start(b_sb[:], b[:, :LATE])
             load_w(e)
-        nc.sync.dma_start(b_late[:], b[:, LATE:])
+            if e in GELUS_BEHIND:
+                group = GELUS_BEHIND[e]
+                t = keep.tile([P, len(group)], F32, name=f"bias{e}")
+                nc.sync.dma_start(t[:], b[:, group.start : group.stop])
+                for done in group:
+                    bias[done] = t[:, done - group.start : done - group.start + 1]
         pos_sb = []
         for r, pos in enumerate((pos1, pos2, pos3)):
             t = keep.tile([P, T // STRIPE], U16, name=f"pos_sb{r}")
@@ -94,18 +103,23 @@ def tile_moe_pkd_lin_gelu_kernel(tc, x_words, x_scales, w, b, gate, offs, pos1, 
         for r in range(TOP):
             nc.sync.dma_start(gate_sb[r][:], gate[r])
 
-        slot_words = []
-        for o in range(PASSES):
-            t = keep.tile([P, SLOTS], U32, name=f"slot_words{o}", align_bytes=256)
-            at = (PASSES - 1 - o) * T
-            for s0 in range(0, SLOTS, CUT):
-                lst = offs_sb[:, s0 // STRIPE : (s0 + CUT) // STRIPE]
-                nc.vector.tensor_copy(t[:, s0 : s0 + CUT], x_all[:, at : at + WINDOW].bitcast(U32).indirect(lst))
-            slot_words.append(t)
+        slot_words = [keep.tile([P, SLOTS], U32, name=f"slot_words{o}", align_bytes=256) for o in range(PASSES)]
         slot_plane = keep.tile([P, SLOTS], U8, name="slot_plane", align_bytes=256)
-        for s0 in range(0, SLOTS, CUT):
+
+        def gather(dst, window, s0):
             lst = offs_sb[:, s0 // STRIPE : (s0 + CUT) // STRIPE]
-            nc.vector.tensor_copy(slot_plane[:, s0 : s0 + CUT], x_plane[:].indirect(lst))
+            nc.vector.tensor_copy(dst[:, s0 : s0 + CUT], window.indirect(lst))
+
+        def gather_words(passes):
+            for s0 in range(0, SLOTS, CUT):
+                for o in passes:
+                    gather(slot_words[o], x_all[:, o * T : o * T + WINDOW].bitcast(U32), s0)
+
+        gather_words([3])
+        for s0 in range(0, SLOTS, CUT):
+            gather(slot_plane, x_plane[:], s0)
+        gather_words([2])
+        gather_words([1, 0])
 
         banks = [psum.tile([N, BANK_OF.count(i) * C], F32, name=f"bank{i}") for i in range(max(BANK_OF) + 1)]
         sums = [banks[BANK_OF[e]][:, (e - BANK_OF.index(BANK_OF[e])) * C : (e - BANK_OF.index(BANK_OF[e]) + 1) * C] for e in range(E)]
@@ -116,64 +130,79 @@ def tile_moe_pkd_lin_gelu_kernel(tc, x_words, x_scales, w, b, gate, offs, pos1, 
                 src.rearrange("p o j (c i) -> p o c j i", i=RUN),
             )
 
-        def quantize_and_multiply(e, grouped, codes, plane, o0, n_pass):
+        def quantize(grouped, codes, plane, o0, n_pass):
             cols = slice(o0 * N, (o0 + n_pass) * N)
             nc.vector.quantize_mx(
                 codes[:, cols].bitcast(FP8X4),
                 plane[:, cols],
                 grouped[:, o0 : o0 + n_pass].rearrange("p o n j -> p (o n j)"),
             )
-            for o in range(o0, o0 + n_pass):
+
+        def multiply(e, codes, plane, at, passes):
+            for o in passes:
+                cols = slice((at + o) * N, (at + o + 1) * N)
                 nc.tensor.matmul_mx(
                     sums[e],
-                    lhsT=codes[:, o * N : (o + 1) * N].bitcast(FP8X4),
-                    lhsT_scale=plane[:, o * N : (o + 1) * N],
+                    lhsT=codes[:, cols].bitcast(FP8X4),
+                    lhsT_scale=plane[:, cols],
                     rhs=slot_words[o][:, e * C : (e + 1) * C].bitcast(FP8X4),
                     rhs_scale=slot_plane[4 * o : P, e * C : (e + 1) * C],
                     start=(o == 0),
                     stop=(o == PASSES - 1),
                 )
 
-        def gelu(e):
-            bias = b_sb[:, e : e + 1] if e < LATE else b_late[:, e - LATE : e - LATE + 1]
-            nc.scalar.activation(y[:, e * C : (e + 1) * C], sums[e], GELU, bias=bias)
+        y = keep.tile([P, SLOTS], F32, name="y", align_bytes=256)
 
-        for e in range(E):
-            reuse = e - 2
-            tag = f"raw{reuse}_0" if 1 <= reuse < HELD else f"grouped{e % 3}"
-            grouped = stage.tile([P, PASSES, N, PACK], BF16, name=f"grouped{e}", tag=tag, align_bytes=256)
-            codes = keep.tile([P, PASSES * N], U32, name=f"codes{e}", align_bytes=64)
-            plane = keep.tile([P, PASSES * N], U8, name=f"plane{e}", align_bytes=64)
+        def gelu(e):
+            nc.scalar.activation(y[:, e * C : (e + 1) * C], sums[e], GELU, bias=bias[e])
+
+        def operand_tiles(e, n_pass, tag):
+            grouped = stage.tile([P, n_pass, N, PACK], BF16, name=f"grouped{e}", tag=tag, align_bytes=256)
+            codes = keep.tile([P, n_pass * N], U32, name=f"codes{e}", align_bytes=64)
+            plane = keep.tile([P, n_pass * N], U8, name=f"plane{e}", align_bytes=64)
+            return grouped, codes, plane
+
+        def raw_passes(e, o0, o1):
             n_pass = PASSES // pieces(e)
+            return raw[e, o0 // n_pass][:, o0 % n_pass : o0 % n_pass + o1 - o0]
+
+        def round_on(engine_copy, e, grouped, at, o0, o1):
+            cast(engine_copy, grouped[:, at + o0 : at + o1], raw_passes(e, o0, o1))
+
+        for e0 in range(0, PAIRED, 2):
+            grouped, codes, plane = operand_tiles(e0, 2 * PASSES, f"raw{e0 // 2 - 1}_0" if e0 > 0 else "first_pair")
+            for k in range(2):
+                n_pass = PASSES // pieces(e0 + k)
+                for o0 in range(0, PASSES, n_pass):
+                    round_on(nc.scalar.copy, e0 + k, grouped, k * PASSES, o0, o0 + n_pass)
+            quantize(grouped, codes, plane, 0, 2 * PASSES)
+            for k in range(2):
+                multiply(e0 + k, codes, plane, k * PASSES, range(PASSES))
+
+        for e in range(PAIRED, E):
+            grouped, codes, plane = operand_tiles(e, PASSES, f"raw{e - 5}_0")
             if e < LAST:
-                engine_copy = nc.vector.tensor_copy if e in ON_VECTOR else nc.scalar.copy
-                if e == LATE:
-                    cast(nc.scalar.copy, grouped[:, 1:], raw[e, 0][:, 1:])
-                    cast(nc.vector.tensor_copy, grouped[:, :1], raw[e, 0][:, :1])
-                else:
-                    for piece in range(pieces(e)):
-                        cast(engine_copy, grouped[:, piece * n_pass : (piece + 1) * n_pass], raw[e, piece][:])
-                quantize_and_multiply(e, grouped, codes, plane, 0, PASSES)
-                if e == HELD:
-                    y = stage.tile([P, SLOTS], F32, name="y", tag=f"raw{e}_0", align_bytes=256)
-                    for done in range(9):
-                        gelu(done)
-                if e == 12:
-                    for done in range(9, 12):
-                        gelu(done)
+                for engine_copy, o0, o1 in [(nc.vector.tensor_copy if on_vector else nc.scalar.copy, a, z) for on_vector, a, z in SHARES[e]]:
+                    round_on(engine_copy, e, grouped, 0, o0, o1)
+                step = 2 if e == LAST - 1 else PASSES
+                for o0 in range(0, PASSES, step):
+                    quantize(grouped, codes, plane, o0, step)
+                    multiply(e, codes, plane, 0, range(o0, o0 + step))
             else:
                 for o in range(PASSES - 1):
-                    cast(nc.scalar.copy, grouped[:, o : o + 1], raw[e, o][:])
-                    quantize_and_multiply(e, grouped, codes, plane, o, 1)
+                    round_on(nc.scalar.copy, e, grouped, 0, o, o + 1)
+                    quantize(grouped, codes, plane, o, 1)
+                    multiply(e, codes, plane, 0, [o])
                 o, half = PASSES - 1, N // 2
                 cast(nc.scalar.copy, grouped[:, o:, :half, :], raw[e, o][:, :, :, :half])
                 cast(nc.vector.tensor_copy, grouped[:, o:, half:, :], raw[e, o][:, :, :, half:])
-                quantize_and_multiply(e, grouped, codes, plane, o, 1)
-                for done in range(12, E):
-                    gelu(done)
+                quantize(grouped, codes, plane, o, 1)
+                multiply(e, codes, plane, 0, [o])
+            for done in GELUS_BEHIND.get(e, []):
+                gelu(done)
 
         first, second, every = slice(0, FIRST_TOKENS), slice(FIRST_TOKENS, T), slice(0, T)
-        free_tags = [f"raw{e}_0" for e in range(1, HELD)]
+        free_tags = [f"raw{e}_{k}" for e in range(5, 11) for k in range(2)]
 
         def scratch(name, span):
             tag = free_tags.pop() if free_tags else name

@@ -27,16 +27,12 @@ RUN = 2
 WINDOW = 2 * T
 CUT = SLOTS // 2
 LAST = E - 1
-SHARES = {
-    10: [(False, 0, 2), (False, 2, 4)],
-    11: [(False, 0, 2), (False, 2, 4)],
-    12: [(True, 0, 4)],
-    13: [(False, 0, 2), (True, 2, 4)],
-}
 X_BEFORE = {0: (3, 4), 3: (2, 3), 5: (0, 2)}
 HALVED = (5, 6, 7, 8, 9, 10, 11, 13)
 PAIRED = 10
-GELUS_BEHIND = {11: range(0, 12), 14: range(12, 15)}
+SMALL_BEHIND = 2
+HELD = 11
+LAST_ORDER = (1, 0, 2, 3)
 FIRST_TOKENS = 384
 BANK_OF = [0, 0, 0, 0, 1, 1, 1, 1, 2, 2, 2, 2, 3, 3, 4]
 
@@ -74,13 +70,14 @@ def tile_moe_pkd_lin_gelu_kernel(tc, x_words, x_scales, w, b, gate, offs, pos1, 
 
         def load_w(e):
             n_pass = PASSES // pieces(e)
-            for piece in range(pieces(e)):
+            for piece in LAST_ORDER if e == LAST else range(pieces(e)):
                 t = stage.tile([P, n_pass, PACK, N], F32, name=f"raw{e}_{piece}", tag=f"raw{e}_{piece}", align_bytes=256)
                 rows = w[e, piece * n_pass * P * PACK : (piece + 1) * n_pass * P * PACK, :]
                 nc.sync.dma_start(t[:], rows.rearrange("(o p j) n -> p o j n", p=P, j=PACK))
                 raw[e, piece] = t
 
-        bias = {}
+        b_sb = keep.tile([P, E], F32, name="b_sb")
+        pos_sb = [keep.tile([P, T // STRIPE], U16, name=f"pos_sb{r}") for r in range(TOP)]
         for e in range(E):
             if e in X_BEFORE:
                 load_x(*X_BEFORE[e])
@@ -88,17 +85,10 @@ def tile_moe_pkd_lin_gelu_kernel(tc, x_words, x_scales, w, b, gate, offs, pos1, 
                 for q in range(4):
                     nc.sync.dma_start(x_plane[32 * q : 32 * q + 16, :T].bitcast(I32), scales_hbm[:, 4 * q : 4 * q + 4, :])
             load_w(e)
-            if e in GELUS_BEHIND:
-                group = GELUS_BEHIND[e]
-                t = keep.tile([P, len(group)], F32, name=f"bias{e}")
-                nc.sync.dma_start(t[:], b[:, group.start : group.stop])
-                for done in group:
-                    bias[done] = t[:, done - group.start : done - group.start + 1]
-        pos_sb = []
-        for r, pos in enumerate((pos1, pos2, pos3)):
-            t = keep.tile([P, T // STRIPE], U16, name=f"pos_sb{r}")
-            nc.sync.dma_start(t[:], pos)
-            pos_sb.append(t)
+            if e == SMALL_BEHIND:
+                nc.sync.dma_start(b_sb[:], b)
+                for t, pos in zip(pos_sb, (pos1, pos2, pos3)):
+                    nc.sync.dma_start(t[:], pos)
         gate_sb = [keep.tile([P, T], F32, name=f"gate_sb{r}", align_bytes=256) for r in range(TOP)]
         for r in range(TOP):
             nc.sync.dma_start(gate_sb[r][:], gate[r])
@@ -147,14 +137,12 @@ def tile_moe_pkd_lin_gelu_kernel(tc, x_words, x_scales, w, b, gate, offs, pos1, 
                     lhsT_scale=plane[:, cols],
                     rhs=slot_words[o][:, e * C : (e + 1) * C].bitcast(FP8X4),
                     rhs_scale=slot_plane[4 * o : P, e * C : (e + 1) * C],
-                    start=(o == 0),
+                    start=(o == (LAST_ORDER[0] if e == LAST else 0)),
                     stop=(o == PASSES - 1),
                 )
 
-        y = keep.tile([P, SLOTS], F32, name="y", align_bytes=256)
-
         def gelu(e):
-            nc.scalar.activation(y[:, e * C : (e + 1) * C], sums[e], GELU, bias=bias[e])
+            nc.scalar.activation(y[:, e * C : (e + 1) * C], sums[e], GELU, bias=b_sb[:, e : e + 1])
 
         def operand_tiles(e, n_pass, tag):
             grouped = stage.tile([P, n_pass, N, PACK], BF16, name=f"grouped{e}", tag=tag, align_bytes=256)
@@ -179,27 +167,43 @@ def tile_moe_pkd_lin_gelu_kernel(tc, x_words, x_scales, w, b, gate, offs, pos1, 
             for k in range(2):
                 multiply(e0 + k, codes, plane, k * PASSES, range(PASSES))
 
-        for e in range(PAIRED, E):
+        for e in range(PAIRED, HELD + 1):
             grouped, codes, plane = operand_tiles(e, PASSES, f"raw{e - 5}_0")
-            if e < LAST:
-                for engine_copy, o0, o1 in [(nc.vector.tensor_copy if on_vector else nc.scalar.copy, a, z) for on_vector, a, z in SHARES[e]]:
-                    round_on(engine_copy, e, grouped, 0, o0, o1)
-                step = 2 if e == LAST - 1 else PASSES
-                for o0 in range(0, PASSES, step):
-                    quantize(grouped, codes, plane, o0, step)
-                    multiply(e, codes, plane, 0, range(o0, o0 + step))
+            for o0 in (0, 2):
+                round_on(nc.scalar.copy, e, grouped, 0, o0, o0 + 2)
+            quantize(grouped, codes, plane, 0, PASSES)
+            multiply(e, codes, plane, 0, range(PASSES))
+        y = stage.tile([P, SLOTS], F32, name="y", tag=f"raw{HELD}_1", align_bytes=256)
+        for e in range(HELD + 1):
+            gelu(e)
+
+        e = HELD + 1
+        grouped, codes, plane = operand_tiles(e, PASSES, f"raw{e - 5}_0")
+        round_on(nc.vector.tensor_copy, e, grouped, 0, 0, PASSES)
+        quantize(grouped, codes, plane, 0, PASSES)
+        multiply(e, codes, plane, 0, range(PASSES))
+
+        e = LAST - 1
+        grouped, codes, plane = operand_tiles(e, 2 * PASSES, "raw4_0")
+        round_on(nc.scalar.copy, e, grouped, 0, 0, 2)
+        round_on(nc.vector.tensor_copy, e, grouped, 0, 2, 4)
+        quantize(grouped, codes, plane, 0, 2)
+        multiply(e, codes, plane, 0, range(2))
+        for o in LAST_ORDER[:-1]:
+            round_on(nc.scalar.copy, LAST, grouped, PASSES, o, o + 1)
+            if o == 0:
+                quantize(grouped, codes, plane, 2, 3)
+                multiply(e, codes, plane, 0, range(2, PASSES))
             else:
-                for o in range(PASSES - 1):
-                    round_on(nc.scalar.copy, e, grouped, 0, o, o + 1)
-                    quantize(grouped, codes, plane, o, 1)
-                    multiply(e, codes, plane, 0, [o])
-                o, half = PASSES - 1, N // 2
-                cast(nc.scalar.copy, grouped[:, o:, :half, :], raw[e, o][:, :, :, :half])
-                cast(nc.vector.tensor_copy, grouped[:, o:, half:, :], raw[e, o][:, :, :, half:])
-                quantize(grouped, codes, plane, o, 1)
-                multiply(e, codes, plane, 0, [o])
-            for done in GELUS_BEHIND.get(e, []):
-                gelu(done)
+                quantize(grouped, codes, plane, PASSES + o, 1)
+            multiply(LAST, codes, plane, PASSES, [o])
+        o, half = PASSES - 1, N // 2
+        cast(nc.scalar.copy, grouped[:, PASSES + o :, :half, :], raw[LAST, o][:, :, :, :half])
+        cast(nc.vector.tensor_copy, grouped[:, PASSES + o :, half:, :], raw[LAST, o][:, :, :, half:])
+        quantize(grouped, codes, plane, PASSES + o, 1)
+        multiply(LAST, codes, plane, PASSES, [o])
+        for e in range(HELD + 1, E):
+            gelu(e)
 
         first, second, every = slice(0, FIRST_TOKENS), slice(FIRST_TOKENS, T), slice(0, T)
         free_tags = [f"raw{e}_{k}" for e in range(5, 11) for k in range(2)]

@@ -33,7 +33,6 @@ PAIRED = 10
 SMALL_BEHIND = 2
 HELD = 11
 LAST_ORDER = (1, 0, 2, 3)
-FIRST_TOKENS = 384
 BANK_OF = [0, 0, 0, 0, 1, 1, 1, 1, 2, 2, 2, 2, 3, 3, 4]
 
 
@@ -87,8 +86,8 @@ def tile_moe_pkd_lin_gelu_kernel(tc, x_words, x_scales, w, b, gate, offs, pos1, 
             load_w(e)
             if e == SMALL_BEHIND:
                 nc.sync.dma_start(b_sb[:], b)
-                for t, pos in zip(pos_sb, (pos1, pos2, pos3)):
-                    nc.sync.dma_start(t[:], pos)
+        for t, pos in zip(pos_sb, (pos1, pos2, pos3)):
+            nc.sync.dma_start(t[:], pos)
         gate_sb = [keep.tile([P, T], F32, name=f"gate_sb{r}", align_bytes=256) for r in range(TOP)]
         for r in range(TOP):
             nc.sync.dma_start(gate_sb[r][:], gate[r])
@@ -169,8 +168,12 @@ def tile_moe_pkd_lin_gelu_kernel(tc, x_words, x_scales, w, b, gate, offs, pos1, 
 
         for e in range(PAIRED, HELD + 1):
             grouped, codes, plane = operand_tiles(e, PASSES, f"raw{e - 5}_0")
-            for o0 in (0, 2):
-                round_on(nc.scalar.copy, e, grouped, 0, o0, o0 + 2)
+            round_on(nc.scalar.copy, e, grouped, 0, 0, 2)
+            if e < HELD:
+                round_on(nc.scalar.copy, e, grouped, 0, 2, 4)
+            else:
+                round_on(nc.scalar.copy, e, grouped, 0, 2, 3)
+                round_on(nc.vector.tensor_copy, e, grouped, 0, 3, 4)
             quantize(grouped, codes, plane, 0, PASSES)
             multiply(e, codes, plane, 0, range(PASSES))
         y = stage.tile([P, SLOTS], F32, name="y", tag=f"raw{HELD}_1", align_bytes=256)
@@ -187,13 +190,13 @@ def tile_moe_pkd_lin_gelu_kernel(tc, x_words, x_scales, w, b, gate, offs, pos1, 
         grouped, codes, plane = operand_tiles(e, 2 * PASSES, "raw4_0")
         round_on(nc.scalar.copy, e, grouped, 0, 0, 2)
         round_on(nc.vector.tensor_copy, e, grouped, 0, 2, 4)
-        quantize(grouped, codes, plane, 0, 2)
-        multiply(e, codes, plane, 0, range(2))
+        quantize(grouped, codes, plane, 0, PASSES - 1)
+        multiply(e, codes, plane, 0, range(PASSES - 1))
         for o in LAST_ORDER[:-1]:
             round_on(nc.scalar.copy, LAST, grouped, PASSES, o, o + 1)
             if o == 0:
-                quantize(grouped, codes, plane, 2, 3)
-                multiply(e, codes, plane, 0, range(2, PASSES))
+                quantize(grouped, codes, plane, PASSES - 1, 2)
+                multiply(e, codes, plane, 0, [PASSES - 1])
             else:
                 quantize(grouped, codes, plane, PASSES + o, 1)
             multiply(LAST, codes, plane, PASSES, [o])
@@ -205,40 +208,45 @@ def tile_moe_pkd_lin_gelu_kernel(tc, x_words, x_scales, w, b, gate, offs, pos1, 
         for e in range(HELD + 1, E):
             gelu(e)
 
-        first, second, every = slice(0, FIRST_TOKENS), slice(FIRST_TOKENS, T), slice(0, T)
-        free_tags = [f"raw{e}_{k}" for e in range(5, 11) for k in range(2)]
-
-        def scratch(name, span):
-            tag = free_tags.pop() if free_tags else name
-            return stage.tile([P, span.stop - span.start], F32, name=name, tag=tag, align_bytes=256)
+        spans = [slice(0, 256), slice(256, 512), slice(512, T)]
+        every = slice(0, T)
 
         def looked_up(r, span):
             return y[:].indirect(pos_sb[r][:, span.start // STRIPE : span.stop // STRIPE])
 
-        def fetch(name, r, span):
-            t = scratch(name, span)
-            nc.scalar.activation(t[:], looked_up(r, span), COPY)
-            return t[:]
+        def token_tile(name, tag):
+            return stage.tile([P, T], F32, name=name, tag=tag, align_bytes=256)
 
-        def product(name, src, r, span):
-            t = scratch(name, span)
-            nc.vector.tensor_tensor(t[:], src, gate_sb[r][:, span], MULT)
-            return t[:]
+        got = {r: token_tile(f"got{r}", f"raw{4 + r}_1") for r in (1, 2)}
+        prod = [token_tile(f"prod{r}", f"raw{7 + r}_1") for r in range(TOP)]
+        part = token_tile("part", "raw10_0")
+        res = token_tile("res", "raw10_1")
 
-        def add(name, left, right, span):
-            t = scratch(name, span)
-            nc.vector.tensor_tensor(t[:], left, right, ADD)
-            return t[:]
+        def product(r, span):
+            src = looked_up(r, span) if r == 0 else got[r][:, span]
+            nc.vector.tensor_tensor(prod[r][:, span], src, gate_sb[r][:, span], MULT)
 
-        got1_first = fetch("got1_first", 1, first)
-        got2_first = fetch("got2_first", 2, first)
-        got2_second = fetch("got2_second", 2, second)
-        prod0 = product("prod0", looked_up(0, every), 0, every)
-        prod1_second = product("prod1_second", looked_up(1, second), 1, second)
-        prod1_first = product("prod1_first", got1_first, 1, first)
-        part_second = add("part_second", prod0[:, second], prod1_second, second)
-        part_first = add("part_first", prod0[:, first], prod1_first, first)
-        prod2_first = product("prod2_first", got2_first, 2, first)
-        prod2_second = product("prod2_second", got2_second, 2, second)
-        nc.sync.dma_start(out[:, first], add("res_first", part_first, prod2_first, first))
-        nc.sync.dma_start(out[:, second], add("res_second", part_second, prod2_second, second))
+        def first_sum(span):
+            nc.vector.tensor_tensor(part[:, span], prod[0][:, span], prod[1][:, span], ADD)
+
+        def finish(span):
+            nc.vector.tensor_tensor(res[:, span], part[:, span], prod[2][:, span], ADD)
+            nc.sync.dma_start(out[:, span], res[:, span])
+
+        for span in spans:
+            for r in (1, 2):
+                nc.scalar.activation(got[r][:, span], looked_up(r, span), COPY)
+        a, bb, c = spans
+        product(0, every)
+        product(1, a)
+        product(2, a)
+        first_sum(a)
+        product(1, bb)
+        finish(a)
+        product(2, bb)
+        first_sum(bb)
+        product(1, c)
+        product(2, c)
+        first_sum(c)
+        finish(bb)
+        finish(c)

@@ -86,10 +86,12 @@ def tile_moe_pkd_lin_gelu_kernel(tc, x_words, x_scales, w, b, gate, offs, pos1, 
             load_w(e)
             if e == SMALL_BEHIND:
                 nc.sync.dma_start(b_sb[:], b)
-        for t, pos in zip(pos_sb, (pos1, pos2, pos3)):
-            nc.sync.dma_start(t[:], pos)
+                nc.sync.dma_start(pos_sb[0][:], pos1)
         gate_sb = [keep.tile([P, T], F32, name=f"gate_sb{r}", align_bytes=256) for r in range(TOP)]
-        for r in range(TOP):
+        nc.sync.dma_start(gate_sb[0][:], gate[0])
+        nc.sync.dma_start(pos_sb[1][:], pos2)
+        nc.sync.dma_start(pos_sb[2][:], pos3)
+        for r in range(1, TOP):
             nc.sync.dma_start(gate_sb[r][:], gate[r])
 
         slot_words = [keep.tile([P, SLOTS], U32, name=f"slot_words{o}", align_bytes=256) for o in range(PASSES)]
@@ -233,20 +235,21 @@ def tile_moe_pkd_lin_gelu_kernel(tc, x_words, x_scales, w, b, gate, offs, pos1, 
             nc.vector.tensor_tensor(res[:, span], part[:, span], prod[2][:, span], ADD)
             nc.sync.dma_start(out[:, span], res[:, span])
 
+        def fetch(r, span):
+            nc.scalar.activation(got[r][:, span], looked_up(r, span), COPY)
+
+        halves = [slice(0, T // 2), slice(T // 2, T)]
+        for span in halves:
+            fetch(1, span)
         for span in spans:
-            for r in (1, 2):
-                nc.scalar.activation(got[r][:, span], looked_up(r, span), COPY)
-        a, bb, c = spans
+            fetch(2, span)
         product(0, every)
-        product(1, a)
-        product(2, a)
-        first_sum(a)
-        product(1, bb)
-        finish(a)
-        product(2, bb)
-        first_sum(bb)
-        product(1, c)
-        product(2, c)
-        first_sum(c)
-        finish(bb)
-        finish(c)
+        for span in halves:
+            product(1, span)
+        for span in halves:
+            first_sum(span)
+        product(2, spans[0])
+        for k, span in enumerate(spans):
+            if k + 1 < len(spans):
+                product(2, spans[k + 1])
+            finish(span)

@@ -47,16 +47,17 @@ def tile_moe_pkd_lin_gelu_kernel(tc, x_words, x_scales, w, b, gate, offs, pos1, 
         nc.sync.dma_start(offs_sb[:], offs)
 
         x_plane = keep.tile([P, WINDOW], U8, name="x_plane", align_bytes=256)
-        nc.vector.memset(x_plane[:].bitcast(I32), 0)
+        nc.gpsimd.memset(x_plane[:].bitcast(I32), 0)
+        for q in range(4):
+            nc.gpsimd.dma_start(x_plane[32 * q : 32 * q + 16, :T].bitcast(I32), x_scales.bitcast(I32)[:, 4 * q : 4 * q + 4, :])
         x_all = keep.tile([P, (PASSES + 1) * T], I32, name="x_all", align_bytes=256)
         nc.vector.memset(x_all[:, PASSES * T :], 0)
 
         warm = keep.tile([P, 16], F32, name="warm")
-        nc.gpsimd.memset(warm[:, :8], 0.0)
+        nc.vector.memset(warm[:, :8], 0.0)
         nc.scalar.activation(warm[:, 8:], warm[:, :8], GELU)
 
         words_hbm = x_words.rearrange("o p t r -> o p (t r)").bitcast(I32)
-        scales_hbm = x_scales.bitcast(I32)
 
         def pieces(e):
             return PASSES if e == LAST else 2 if e in HALVED else 1
@@ -80,9 +81,6 @@ def tile_moe_pkd_lin_gelu_kernel(tc, x_words, x_scales, w, b, gate, offs, pos1, 
         for e in range(E):
             if e in X_BEFORE:
                 load_x(*X_BEFORE[e])
-            if e == 1:
-                for q in range(4):
-                    nc.sync.dma_start(x_plane[32 * q : 32 * q + 16, :T].bitcast(I32), scales_hbm[:, 4 * q : 4 * q + 4, :])
             load_w(e)
             if e == SMALL_BEHIND:
                 nc.sync.dma_start(b_sb[:], b)

@@ -29,6 +29,7 @@ CUT = SLOTS // 2
 LAST = E - 1
 X_BEFORE = {0: (3, 4), 3: (2, 3), 5: (0, 2)}
 HALVED = (5, 6, 7, 8, 9, 10, 11, 13)
+TWO_LOADS = (0, 1, 2, 3, 4, 12)
 PAIRED = 10
 SMALL_BEHIND = 2
 HELD = 11
@@ -72,8 +73,11 @@ def tile_moe_pkd_lin_gelu_kernel(tc, x_words, x_scales, w, b, gate, offs, pos1, 
             n_pass = PASSES // pieces(e)
             for piece in LAST_ORDER if e == LAST else range(pieces(e)):
                 t = stage.tile([P, n_pass, PACK, N], F32, name=f"raw{e}_{piece}", tag=f"raw{e}_{piece}", align_bytes=256)
-                rows = w[e, piece * n_pass * P * PACK : (piece + 1) * n_pass * P * PACK, :]
-                nc.sync.dma_start(t[:], rows.rearrange("(o p j) n -> p o j n", p=P, j=PACK))
+                step = 2 if e in TWO_LOADS else n_pass
+                for o in range(0, n_pass, step):
+                    k0 = (piece * n_pass + o) * P * PACK
+                    rows = w[e, k0 : k0 + step * P * PACK, :]
+                    nc.sync.dma_start(t[:, o : o + step], rows.rearrange("(o p j) n -> p o j n", p=P, j=PACK))
                 raw[e, piece] = t
 
         b_sb = keep.tile([P, E], F32, name="b_sb")
@@ -84,10 +88,10 @@ def tile_moe_pkd_lin_gelu_kernel(tc, x_words, x_scales, w, b, gate, offs, pos1, 
             load_w(e)
             if e == SMALL_BEHIND:
                 nc.sync.dma_start(b_sb[:], b)
-                nc.sync.dma_start(pos_sb[0][:], pos1)
         gate_sb = [keep.tile([P, T], F32, name=f"gate_sb{r}", align_bytes=256) for r in range(TOP)]
-        nc.sync.dma_start(gate_sb[0][:], gate[0])
         nc.sync.dma_start(pos_sb[1][:], pos2)
+        nc.sync.dma_start(pos_sb[0][:], pos1)
+        nc.sync.dma_start(gate_sb[0][:], gate[0])
         nc.sync.dma_start(pos_sb[2][:], pos3)
         for r in range(1, TOP):
             nc.sync.dma_start(gate_sb[r][:], gate[r])
@@ -159,9 +163,8 @@ def tile_moe_pkd_lin_gelu_kernel(tc, x_words, x_scales, w, b, gate, offs, pos1, 
         for e0 in range(0, PAIRED, 2):
             grouped, codes, plane = operand_tiles(e0, 2 * PASSES, f"raw{e0 // 2 - 1}_0" if e0 > 0 else "first_pair")
             for k in range(2):
-                n_pass = PASSES // pieces(e0 + k)
-                for o0 in range(0, PASSES, n_pass):
-                    round_on(nc.scalar.copy, e0 + k, grouped, k * PASSES, o0, o0 + n_pass)
+                for o0 in (0, 2):
+                    round_on(nc.scalar.copy, e0 + k, grouped, k * PASSES, o0, o0 + 2)
             quantize(grouped, codes, plane, 0, 2 * PASSES)
             for k in range(2):
                 multiply(e0 + k, codes, plane, k * PASSES, range(PASSES))
@@ -182,14 +185,17 @@ def tile_moe_pkd_lin_gelu_kernel(tc, x_words, x_scales, w, b, gate, offs, pos1, 
 
         e = HELD + 1
         grouped, codes, plane = operand_tiles(e, PASSES, f"raw{e - 5}_0")
-        round_on(nc.vector.tensor_copy, e, grouped, 0, 0, PASSES)
-        quantize(grouped, codes, plane, 0, PASSES)
+        for o0 in (0, 2):
+            round_on(nc.vector.tensor_copy, e, grouped, 0, o0, o0 + 2)
+        for o0 in (0, 2):
+            quantize(grouped, codes, plane, o0, 2)
         multiply(e, codes, plane, 0, range(PASSES))
 
         e = LAST - 1
         grouped, codes, plane = operand_tiles(e, 2 * PASSES, "raw4_0")
         round_on(nc.scalar.copy, e, grouped, 0, 0, 2)
-        round_on(nc.vector.tensor_copy, e, grouped, 0, 2, 4)
+        for o in (2, 3):
+            round_on(nc.vector.tensor_copy, e, grouped, 0, o, o + 1)
         quantize(grouped, codes, plane, 0, PASSES - 1)
         multiply(e, codes, plane, 0, range(PASSES - 1))
         for o in LAST_ORDER[:-1]:

@@ -27,14 +27,16 @@ RUN = 2
 WINDOW = 2 * T
 CUT = SLOTS // 2
 LAST = E - 1
-X_BEFORE = {0: (3, 4), 3: (2, 3), 5: (0, 2)}
-HALVED = (5, 6, 7, 8, 9, 10, 11, 13)
-TWO_LOADS = (0, 1, 2, 3, 4, 12)
+X_BEFORE = {0: ((3, 4), (0, 3))}
+JOINED = (1, 3)
+HALVED = (6, 7, 8, 9, 10, 11, 13)
+TWO_LOADS = (12,)
+SHARED = 7
 PAIRED = 10
 SMALL_BEHIND = 2
 HELD = 11
 LAST_ORDER = (1, 0, 2, 3)
-BANK_OF = [0, 0, 0, 0, 1, 1, 1, 1, 2, 2, 2, 2, 3, 3, 4]
+BANK_OF = [0, 0, 0, 0, 1, 1, 1, 1, 2, 2, 3, 3, 4, 4, 5]
 
 
 def tile_moe_pkd_lin_gelu_kernel(tc, x_words, x_scales, w, b, gate, offs, pos1, pos2, pos3, out):
@@ -70,6 +72,13 @@ def tile_moe_pkd_lin_gelu_kernel(tc, x_words, x_scales, w, b, gate, offs, pos1, 
             nc.sync.dma_start(dst, words_hbm[o0:o1].rearrange("o p t -> p o t"))
 
         def load_w(e):
+            if e in JOINED:
+                t = stage.tile([P, 2 * PASSES, PACK, N], F32, name=f"raw{e}_0", tag=f"raw{e}_0", align_bytes=256)
+                nc.sync.dma_start(t[:], w[e : e + 2].rearrange("e (o p j) n -> p (e o) j n", p=P, j=PACK))
+                raw[e, 0], raw[e + 1, 0] = t[:, :PASSES], t[:, PASSES:]
+                return
+            if e - 1 in JOINED:
+                return
             n_pass = PASSES // pieces(e)
             for piece in LAST_ORDER if e == LAST else range(pieces(e)):
                 t = stage.tile([P, n_pass, PACK, N], F32, name=f"raw{e}_{piece}", tag=f"raw{e}_{piece}", align_bytes=256)
@@ -83,8 +92,8 @@ def tile_moe_pkd_lin_gelu_kernel(tc, x_words, x_scales, w, b, gate, offs, pos1, 
         b_sb = keep.tile([P, E], F32, name="b_sb")
         pos_sb = [keep.tile([P, T // STRIPE], U16, name=f"pos_sb{r}") for r in range(TOP)]
         for e in range(E):
-            if e in X_BEFORE:
-                load_x(*X_BEFORE[e])
+            for passes in X_BEFORE.get(e, ()):
+                load_x(*passes)
             load_w(e)
             if e == SMALL_BEHIND:
                 nc.sync.dma_start(b_sb[:], b)
@@ -97,7 +106,6 @@ def tile_moe_pkd_lin_gelu_kernel(tc, x_words, x_scales, w, b, gate, offs, pos1, 
             nc.sync.dma_start(gate_sb[r][:], gate[r])
 
         slot_words = [keep.tile([P, SLOTS], U32, name=f"slot_words{o}", align_bytes=256) for o in range(PASSES)]
-        slot_plane = keep.tile([P, SLOTS], U8, name="slot_plane", align_bytes=256)
 
         def gather(dst, window, s0):
             lst = offs_sb[:, s0 // STRIPE : (s0 + CUT) // STRIPE]
@@ -109,10 +117,7 @@ def tile_moe_pkd_lin_gelu_kernel(tc, x_words, x_scales, w, b, gate, offs, pos1, 
                     gather(slot_words[o], x_all[:, o * T : o * T + WINDOW].bitcast(U32), s0)
 
         gather_words([3])
-        for s0 in range(0, SLOTS, CUT):
-            gather(slot_plane, x_plane[:], s0)
         gather_words([2])
-        gather_words([1, 0])
 
         banks = [psum.tile([N, BANK_OF.count(i) * C], F32, name=f"bank{i}") for i in range(max(BANK_OF) + 1)]
         sums = [banks[BANK_OF[e]][:, (e - BANK_OF.index(BANK_OF[e])) * C : (e - BANK_OF.index(BANK_OF[e]) + 1) * C] for e in range(E)]
@@ -160,23 +165,33 @@ def tile_moe_pkd_lin_gelu_kernel(tc, x_words, x_scales, w, b, gate, offs, pos1, 
         def round_on(engine_copy, e, grouped, at, o0, o1):
             cast(engine_copy, grouped[:, at + o0 : at + o1], raw_passes(e, o0, o1))
 
+        def round_on_gpsimd(e, grouped, at, o):
+            src = raw_passes(e, o, o + 1)[:, 0].rearrange("p j n -> p n j")
+            nc.gpsimd.tensor_scalar(grouped[:, at + o], src, 1.0, 0.0, MULT, ADD)
+
         for e0 in range(0, PAIRED, 2):
-            grouped, codes, plane = operand_tiles(e0, 2 * PASSES, f"raw{e0 // 2 - 1}_0" if e0 > 0 else "first_pair")
+            grouped, codes, plane = operand_tiles(e0, 2 * PASSES, ("first_pair", "second_pair", "raw1_0", "raw3_0", "raw5_0")[e0 // 2])
             for k in range(2):
-                for o0 in (0, 2):
-                    round_on(nc.scalar.copy, e0 + k, grouped, k * PASSES, o0, o0 + 2)
+                n_pass = PASSES // pieces(e0 + k)
+                for o0 in range(0, PASSES, n_pass):
+                    if e0 + k < SHARED:
+                        round_on(nc.scalar.copy, e0 + k, grouped, k * PASSES, o0, o0 + n_pass - 1)
+                        round_on_gpsimd(e0 + k, grouped, k * PASSES, o0 + n_pass - 1)
+                    else:
+                        round_on(nc.scalar.copy, e0 + k, grouped, k * PASSES, o0, o0 + n_pass)
+            if e0 == 0:
+                slot_plane = stage.tile([P, SLOTS], U8, name="slot_plane", tag="raw0_0", align_bytes=256)
+                for s0 in range(0, SLOTS, CUT):
+                    gather(slot_plane, x_plane[:], s0)
+                gather_words([1, 0])
             quantize(grouped, codes, plane, 0, 2 * PASSES)
             for k in range(2):
                 multiply(e0 + k, codes, plane, k * PASSES, range(PASSES))
 
         for e in range(PAIRED, HELD + 1):
-            grouped, codes, plane = operand_tiles(e, PASSES, f"raw{e - 5}_0")
+            grouped, codes, plane = operand_tiles(e, PASSES, f"raw7_{e - PAIRED}")
             round_on(nc.scalar.copy, e, grouped, 0, 0, 2)
-            if e < HELD:
-                round_on(nc.scalar.copy, e, grouped, 0, 2, 4)
-            else:
-                round_on(nc.scalar.copy, e, grouped, 0, 2, 3)
-                round_on(nc.vector.tensor_copy, e, grouped, 0, 3, 4)
+            round_on(nc.scalar.copy, e, grouped, 0, 2, 4)
             quantize(grouped, codes, plane, 0, PASSES)
             multiply(e, codes, plane, 0, range(PASSES))
         y = stage.tile([P, SLOTS], F32, name="y", tag=f"raw{HELD}_1", align_bytes=256)
@@ -184,7 +199,7 @@ def tile_moe_pkd_lin_gelu_kernel(tc, x_words, x_scales, w, b, gate, offs, pos1, 
             gelu(e)
 
         e = HELD + 1
-        grouped, codes, plane = operand_tiles(e, PASSES, f"raw{e - 5}_0")
+        grouped, codes, plane = operand_tiles(e, PASSES, "first_pair")
         for o0 in (0, 2):
             round_on(nc.vector.tensor_copy, e, grouped, 0, o0, o0 + 2)
         for o0 in (0, 2):
@@ -192,7 +207,7 @@ def tile_moe_pkd_lin_gelu_kernel(tc, x_words, x_scales, w, b, gate, offs, pos1, 
         multiply(e, codes, plane, 0, range(PASSES))
 
         e = LAST - 1
-        grouped, codes, plane = operand_tiles(e, 2 * PASSES, "raw4_0")
+        grouped, codes, plane = operand_tiles(e, 2 * PASSES, "second_pair")
         round_on(nc.scalar.copy, e, grouped, 0, 0, 2)
         for o in (2, 3):
             round_on(nc.vector.tensor_copy, e, grouped, 0, o, o + 1)
@@ -223,8 +238,8 @@ def tile_moe_pkd_lin_gelu_kernel(tc, x_words, x_scales, w, b, gate, offs, pos1, 
         def token_tile(name, tag):
             return stage.tile([P, T], F32, name=name, tag=tag, align_bytes=256)
 
-        got = {r: token_tile(f"got{r}", f"raw{4 + r}_1") for r in (1, 2)}
-        prod = [token_tile(f"prod{r}", f"raw{7 + r}_1") for r in range(TOP)]
+        got = {r: token_tile(f"got{r}", f"raw8_{r - 1}") for r in (1, 2)}
+        prod = [token_tile(f"prod{r}", ("raw9_0", "raw9_1", "raw11_0")[r]) for r in range(TOP)]
         part = token_tile("part", "raw10_0")
         res = token_tile("res", "raw10_1")
 

from contextlib import ExitStack

import concourse.mybir as mybir

K, T, E, C, N = 2048, 640, 15, 128, 128
TOP = 3
FLOPS = 2 * E * C * K * N

F32 = mybir.dt.float32
BF16 = mybir.dt.bfloat16
I32 = mybir.dt.int32
U32 = mybir.dt.uint32
U16 = mybir.dt.uint16
U8 = mybir.dt.uint8
FP8X4 = mybir.dt.float8_e4m3fn_x4
GELU = mybir.ActivationFunctionType.Gelu_apprx_tanh
COPY = mybir.ActivationFunctionType.Copy
MULT = mybir.AluOpType.mult
ADD = mybir.AluOpType.add

P = 128
PACK = 4
PASSES = K // (P * PACK)
SLOTS = E * C
STRIPE = 16
RUN = 2
WINDOW = 2 * T
CUT = SLOTS // 2
LAST = E - 1
X_BEFORE = {0: ((3, 4), (0, 3))}
JOINED = (1, 3)
HALVED = (6, 7, 8, 9, 10, 11, 13)
TWO_LOADS = (12,)
SHARED = 7
PAIRED = 10
SMALL_BEHIND = 2
HELD = 11
LAST_ORDER = (1, 0, 2, 3)
BANK_OF = [0, 0, 0, 0, 1, 1, 1, 1, 2, 2, 3, 3, 4, 4, 5]


def tile_moe_pkd_lin_gelu_kernel(tc, x_words, x_scales, w, b, gate, offs, pos1, pos2, pos3, out):
    nc = tc.nc
    with ExitStack() as ctx:
        keep = ctx.enter_context(tc.tile_pool(name="keep", bufs=1))
        stage = ctx.enter_context(tc.tile_pool(name="stage", bufs=1))
        psum = ctx.enter_context(tc.psum_pool(name="psum", bufs=1))

        offs_sb = keep.tile([P, SLOTS // STRIPE], U16, name="offs_sb")
        nc.sync.dma_start(offs_sb[:], offs)

        x_plane = keep.tile([P, WINDOW], U8, name="x_plane", align_bytes=256)
        nc.gpsimd.memset(x_plane[:].bitcast(I32), 0)
        for q in range(4):
            nc.gpsimd.dma_start(x_plane[32 * q : 32 * q + 16, :T].bitcast(I32), x_scales.bitcast(I32)[:, 4 * q : 4 * q + 4, :])
        x_all = keep.tile([P, (PASSES + 1) * T], I32, name="x_all", align_bytes=256)
        nc.vector.memset(x_all[:, PASSES * T :], 0)

        warm = keep.tile([P, 16], F32, name="warm")
        nc.vector.memset(warm[:, :8], 0.0)
        nc.scalar.activation(warm[:, 8:], warm[:, :8], GELU)

        words_hbm = x_words.rearrange("o p t r -> o p (t r)").bitcast(I32)

        def pieces(e):
            return PASSES if e == LAST else 2 if e in HALVED else 1

        raw = {}

        def load_x(o0, o1):
            dst = x_all[:, o0 * T : o1 * T].rearrange("p (o t) -> p o t", t=T)
            nc.sync.dma_start(dst, words_hbm[o0:o1].rearrange("o p t -> p o t"))

        def load_w(e):
            if e in JOINED:
                t = stage.tile([P, 2 * PASSES, PACK, N], F32, name=f"raw{e}_0", tag=f"raw{e}_0", align_bytes=256)
                nc.sync.dma_start(t[:], w[e : e + 2].rearrange("e (o p j) n -> p (e o) j n", p=P, j=PACK))
                raw[e, 0], raw[e + 1, 0] = t[:, :PASSES], t[:, PASSES:]
                return
            if e - 1 in JOINED:
                return
            n_pass = PASSES // pieces(e)
            for piece in LAST_ORDER if e == LAST else range(pieces(e)):
                t = stage.tile([P, n_pass, PACK, N], F32, name=f"raw{e}_{piece}", tag=f"raw{e}_{piece}", align_bytes=256)
                step = 2 if e in TWO_LOADS else n_pass
                for o in range(0, n_pass, step):
                    k0 = (piece * n_pass + o) * P * PACK
                    rows = w[e, k0 : k0 + step * P * PACK, :]
                    nc.sync.dma_start(t[:, o : o + step], rows.rearrange("(o p j) n -> p o j n", p=P, j=PACK))
                raw[e, piece] = t

        b_sb = keep.tile([P, E], F32, name="b_sb")
        pos_sb = [keep.tile([P, T // STRIPE], U16, name=f"pos_sb{r}") for r in range(TOP)]
        for e in range(E):
            for passes in X_BEFORE.get(e, ()):
                load_x(*passes)
            load_w(e)
            if e == SMALL_BEHIND:
                nc.sync.dma_start(b_sb[:], b)
        gate_sb = [keep.tile([P, T], F32, name=f"gate_sb{r}", align_bytes=256) for r in range(TOP)]
        nc.sync.dma_start(pos_sb[1][:], pos2)
        nc.sync.dma_start(pos_sb[0][:], pos1)
        nc.sync.dma_start(gate_sb[0][:], gate[0])
        nc.sync.dma_start(pos_sb[2][:], pos3)
        for r in range(1, TOP):
            nc.sync.dma_start(gate_sb[r][:], gate[r])

        slot_words = [keep.tile([P, SLOTS], U32, name=f"slot_words{o}", align_bytes=256) for o in range(PASSES)]

        def gather(dst, window, s0):
            lst = offs_sb[:, s0 // STRIPE : (s0 + CUT) // STRIPE]
            nc.vector.tensor_copy(dst[:, s0 : s0 + CUT], window.indirect(lst))

        def gather_words(passes):
            for s0 in range(0, SLOTS, CUT):
                for o in passes:
                    gather(slot_words[o], x_all[:, o * T : o * T + WINDOW].bitcast(U32), s0)

        gather_words([3])
        gather_words([2])

        banks = [psum.tile([N, BANK_OF.count(i) * C], F32, name=f"bank{i}") for i in range(max(BANK_OF) + 1)]
        sums = [banks[BANK_OF[e]][:, (e - BANK_OF.index(BANK_OF[e])) * C : (e - BANK_OF.index(BANK_OF[e]) + 1) * C] for e in range(E)]

        def cast(engine_copy, dst, src):
            engine_copy(
                dst.rearrange("p o (c i) j -> p o c j i", i=RUN),
                src.rearrange("p o j (c i) -> p o c j i", i=RUN),
            )

        def quantize(grouped, codes, plane, o0, n_pass):
            cols = slice(o0 * N, (o0 + n_pass) * N)
            nc.vector.quantize_mx(
                codes[:, cols].bitcast(FP8X4),
                plane[:, cols],
                grouped[:, o0 : o0 + n_pass].rearrange("p o n j -> p (o n j)"),
            )

        def multiply(e, codes, plane, at, passes):
            for o in passes:
                cols = slice((at + o) * N, (at + o + 1) * N)
                nc.tensor.matmul_mx(
                    sums[e],
                    lhsT=codes[:, cols].bitcast(FP8X4),
                    lhsT_scale=plane[:, cols],
                    rhs=slot_words[o][:, e * C : (e + 1) * C].bitcast(FP8X4),
                    rhs_scale=slot_plane[4 * o : P, e * C : (e + 1) * C],
                    start=(o == (LAST_ORDER[0] if e == LAST else 0)),
                    stop=(o == PASSES - 1),
                )

        def gelu(e):
            nc.scalar.activation(y[:, e * C : (e + 1) * C], sums[e], GELU, bias=b_sb[:, e : e + 1])

        def operand_tiles(e, n_pass, tag):
            grouped = stage.tile([P, n_pass, N, PACK], BF16, name=f"grouped{e}", tag=tag, align_bytes=256)
            codes = keep.tile([P, n_pass * N], U32, name=f"codes{e}", align_bytes=64)
            plane = keep.tile([P, n_pass * N], U8, name=f"plane{e}", align_bytes=64)
            return grouped, codes, plane

        def raw_passes(e, o0, o1):
            n_pass = PASSES // pieces(e)
            return raw[e, o0 // n_pass][:, o0 % n_pass : o0 % n_pass + o1 - o0]

        def round_on(engine_copy, e, grouped, at, o0, o1):
            cast(engine_copy, grouped[:, at + o0 : at + o1], raw_passes(e, o0, o1))

        def round_on_gpsimd(e, grouped, at, o):
            src = raw_passes(e, o, o + 1)[:, 0].rearrange("p j n -> p n j")
            nc.gpsimd.tensor_scalar(grouped[:, at + o], src, 1.0, 0.0, MULT, ADD)

        for e0 in range(0, PAIRED, 2):
            grouped, codes, plane = operand_tiles(e0, 2 * PASSES, ("first_pair", "second_pair", "raw1_0", "raw3_0", "raw5_0")[e0 // 2])
            for k in range(2):
                n_pass = PASSES // pieces(e0 + k)
                for o0 in range(0, PASSES, n_pass):
                    if e0 + k < SHARED:
                        round_on(nc.scalar.copy, e0 + k, grouped, k * PASSES, o0, o0 + n_pass - 1)
                        round_on_gpsimd(e0 + k, grouped, k * PASSES, o0 + n_pass - 1)
                    else:
                        round_on(nc.scalar.copy, e0 + k, grouped, k * PASSES, o0, o0 + n_pass)
            if e0 == 0:
                slot_plane = stage.tile([P, SLOTS], U8, name="slot_plane", tag="raw0_0", align_bytes=256)
                for s0 in range(0, SLOTS, CUT):
                    gather(slot_plane, x_plane[:], s0)
                gather_words([1, 0])
            quantize(grouped, codes, plane, 0, 2 * PASSES)
            for k in range(2):
                multiply(e0 + k, codes, plane, k * PASSES, range(PASSES))

        for e in range(PAIRED, HELD + 1):
            grouped, codes, plane = operand_tiles(e, PASSES, f"raw7_{e - PAIRED}")
            round_on(nc.scalar.copy, e, grouped, 0, 0, 2)
            round_on(nc.scalar.copy, e, grouped, 0, 2, 4)
            quantize(grouped, codes, plane, 0, PASSES)
            multiply(e, codes, plane, 0, range(PASSES))
        y = stage.tile([P, SLOTS], F32, name="y", tag=f"raw{HELD}_1", align_bytes=256)
        for e in range(HELD + 1):
            gelu(e)

        e = HELD + 1
        grouped, codes, plane = operand_tiles(e, PASSES, "first_pair")
        for o0 in (0, 2):
            round_on(nc.vector.tensor_copy, e, grouped, 0, o0, o0 + 2)
        for o0 in (0, 2):
            quantize(grouped, codes, plane, o0, 2)
        multiply(e, codes, plane, 0, range(PASSES))

        e = LAST - 1
        grouped, codes, plane = operand_tiles(e, 2 * PASSES, "second_pair")
        round_on(nc.scalar.copy, e, grouped, 0, 0, 2)
        for o in (2, 3):
            round_on(nc.vector.tensor_copy, e, grouped, 0, o, o + 1)
        quantize(grouped, codes, plane, 0, PASSES - 1)
        multiply(e, codes, plane, 0, range(PASSES - 1))
        for o in LAST_ORDER[:-1]:
            round_on(nc.scalar.copy, LAST, grouped, PASSES, o, o + 1)
            if o == 0:
                quantize(grouped, codes, plane, PASSES - 1, 2)
                multiply(e, codes, plane, 0, [PASSES - 1])
            else:
                quantize(grouped, codes, plane, PASSES + o, 1)
            multiply(LAST, codes, plane, PASSES, [o])
        o, half = PASSES - 1, N // 2
        cast(nc.scalar.copy, grouped[:, PASSES + o :, :half, :], raw[LAST, o][:, :, :, :half])
        cast(nc.vector.tensor_copy, grouped[:, PASSES + o :, half:, :], raw[LAST, o][:, :, :, half:])
        quantize(grouped, codes, plane, PASSES + o, 1)
        multiply(LAST, codes, plane, PASSES, [o])
        for e in range(HELD + 1, E):
            gelu(e)

        spans = [slice(0, 256), slice(256, 512), slice(512, T)]
        every = slice(0, T)

        def looked_up(r, span):
            return y[:].indirect(pos_sb[r][:, span.start // STRIPE : span.stop // STRIPE])

        def token_tile(name, tag):
            return stage.tile([P, T], F32, name=name, tag=tag, align_bytes=256)

        got = {r: token_tile(f"got{r}", f"raw8_{r - 1}") for r in (1, 2)}
        prod = [token_tile(f"prod{r}", ("raw9_0", "raw9_1", "raw11_0")[r]) for r in range(TOP)]
        part = token_tile("part", "raw10_0")
        res = token_tile("res", "raw10_1")

        def product(r, span):
            src = looked_up(r, span) if r == 0 else got[r][:, span]
            nc.vector.tensor_tensor(prod[r][:, span], src, gate_sb[r][:, span], MULT)

        def first_sum(span):
            nc.vector.tensor_tensor(part[:, span], prod[0][:, span], prod[1][:, span], ADD)

        def finish(span):
            nc.vector.tensor_tensor(res[:, span], part[:, span], prod[2][:, span], ADD)
            nc.sync.dma_start(out[:, span], res[:, span])

        def fetch(r, span):
            nc.scalar.activation(got[r][:, span], looked_up(r, span), COPY)

        halves = [slice(0, T // 2), slice(T // 2, T)]
        for span in halves:
            fetch(1, span)
        for span in spans:
            fetch(2, span)
        product(0, every)
        for span in halves:
            product(1, span)
        for span in halves:
            first_sum(span)
        product(2, spans[0])
        for k, span in enumerate(spans):
            if k + 1 < len(spans):
                product(2, spans[k + 1])
            finish(span)
